import numpy as np, ml_dtypes
CORES = [36,164,52,180,100,228,116,244]
N = 8
BF = ml_dtypes.bfloat16
def gentries(a):
    return np.ascontiguousarray(a.reshape(8, 16, -1).transpose(0, 2, 1)).reshape(8, -1)
def gtable(e):
    e = np.asarray(e); return np.ascontiguousarray(e.reshape(8, -1, 16).transpose(0, 2, 1)).reshape(128, -1).astype(np.int32)
V, T, J, CAP, RO, M, LN = 1536, 256, 6, 16, 2, 3, 3
E = N * CAP * J; A = V + RO * E; F = 2 * J + 2
def codes(rng, back):
    u = rng.random((N, 8, 16, T))
    c = np.where(u < 0.15, 0, np.where(u < 0.5, rng.integers(1, J + 1, u.shape), J + back))
    c[:, :, F:] = 0; c[:, :, F] = rng.integers(1, J + 1, (N, 8, T))
    return c
def parts(rng):
    x = rng.integers(0, 16, (N, 8, 16, V)); kd = np.where(rng.random((N, 8, 2, V)) < 0.25, A, rng.integers(0, V, (N, 8, 2, V)))
    wt = rng.integers(0, 256, (N, 8, 16)); wt[..., 0] |= 1
    th = rng.integers(40, 81, (N, 8))
    for q in range(N):
        o = rng.permutation(8); th[q, o[0]] = 42; th[q, o[1]] = 80
    rx = rng.integers(0, 16, (N, 8, 16, T)); nx = rng.integers(0, 16, (N, 8, 16, J, T)); tk = codes(rng, rng.integers(1, V + 1, (N, 8, 16, T)))
    return x, kd, wt, th, rx, nx, tk
def small(a, n):
    return np.ascontiguousarray(a.reshape(N, 128, n)).astype(np.float32).astype(BF)
def pack(x, kd, wt, th, rx, nx, tk):
    return {"x0": small(x, V), "k0": np.stack([gtable(a) for a in kd[:, :, 0]]), "k1": np.stack([gtable(a) for a in kd[:, :, 1]]),
            "wt": wt.reshape(N, 128, 1).astype(np.int32), "th": np.repeat(th, 16, axis=1).reshape(N, 128, 1).astype(np.int32),
            "rx": small(rx, T), "nx": small(nx, J * T), "tk": np.ascontiguousarray(tk.reshape(N, 128, T)).astype(np.int32)}
def setup_inputs(rng):
    return pack(*parts(rng))
def setup_inputs_alike(rng):
    x, kd, wt, th, rx, nx, tk = parts(rng); v = np.arange(V)
    wt[:, ::2] = 0; th[:, ::2] = 70; th[:, ::4] = 241; th[:, 5] = 241
    kd[:, 1] = v; kd[:, 2, 0] = 0; kd[:, 2, 1] = V - 1; kd[:, 3] = np.where(v < V - 1, v + 1, A)
    x[:, 5] = np.tile(x[:, 5, :, :4], (1, 1, V // 4))
    tk[:, 4, :F] = 0; tk[:, 5, :F] = 1; tk[:, 6, :F] = rng.choice(np.array([J + 1, J + V]), (N, F, T)); tk[:, 7, :F] = rng.integers(1, J + 1, (N, F, T))
    tk[:, 0, F] = 1; tk[:, 1, F] = J
    return pack(x, kd, wt, th, rx, nx, tk)
def setup_inputs_edge(rng):
    x, kd, wt, th, rx, nx, tk = parts(rng)
    rho = rng.integers(2, 6, (8, 16)); th = rng.integers(8, 21, (N, 8))
    rx = np.broadcast_to(rho[None, :, :, None], (N, 8, 16, T)).copy(); rx[:, :, 0] += (rng.random((N, 8, T)) < 0.7).astype(np.int64)
    want = th[:, :, None] - 1 + rng.choice(np.array([-1, 0, 0, 1]), (N, 8, E))
    e = np.argsort(rng.random((N, 8, E, 30)), axis=-1) < want[..., None]
    e = np.add.reduce(e.reshape(N, 8, E, 15, 2).astype(np.int64), axis=-1)
    y = np.broadcast_to(rho[None, :, None, :], (N, 8, E, 16)).copy(); y[..., 1:] += e * rng.choice(np.array([-1, 1]), e.shape)
    x[..., V - E:] = 2 * y.transpose(0, 1, 3, 2) + rng.integers(0, 2, (N, 8, 16, E)); kd[..., V - E:] = A
    nx = rho[None, :, :, None, None] + rng.integers(-1, 2, (N, 8, 16, J, T))
    far = [int(g) for g in rng.permutation(8)[:3]]
    for g in far: kd[:, g, :, V - E:] = np.arange(V - E, V)
    for i in (0, 1):
        g = far[i]; lv = rng.integers(10, 15, N)
        if i == 0: lv[:] = 14
        x[:, g, :, V - E:] = lv[:, None, None] + rng.integers(-1, 2, (N, 16, E)); rx[:, g] = rng.integers(0, 4, (N, 16, T))
        th[:, g] = 16 * lv - 24 + rng.choice(np.array([-5, -3, -1, 1, 3, 5]), N)
    g = far[2]; few = rng.random((N, 1, E)) < 0.5
    x[:, g, :, V - E:] = np.where(few & (rng.random((N, 16, E)) < 0.2), 14, 15); x[:, g, :, V - E] = 15; rx[:, g] = 0
    th[:, g] = np.where(rng.permutation(N) % 2 == 0, 241, 240)
    wt[:, far[0]] = rng.integers(240, 256, (N, 16)); wt[:, far[2]] = rng.integers(240, 256, (N, 16))
    return pack(x, kd, wt, th, rx, nx, tk)
def setup_inputs_quiet(rng):
    x, kd, wt, th, rx, nx, tk = parts(rng)
    q = rng.permutation(N); th[q[1]] = 241; th[:, rng.integers(0, 8)] = 0; th[q[0]] = 0
    return pack(x, kd, wt, th, rx, nx, tk)
def setup_inputs_room(rng):
    x, kd, wt, th, rx, nx, tk = parts(rng)
    wt[:] = 0; wt[..., 0] = 1; wt[..., 1] = 8; wt[..., 2] = 64
    rx[:, :, 3:] = 0; th[:] = 50; kd[..., V - E:] = A
    for q in range(N):
        for g in range(8):
            n = rng.choice(np.array([0, 1, CAP - 1, CAP, CAP + 1, 2 * CAP]), N)
            if q == 0: n[1] = (CAP, CAP + 1, 0, CAP - 1, 1, 2 * CAP, CAP, CAP + 1)[g]
            own = np.concatenate([np.repeat(np.arange(N), n), np.full(E - int(np.sum(n)), -1)])
            own = rng.permutation(own)
            y = rng.integers(0, 8, (16, E)); y[3:] = np.where(own >= 0, 0, rng.integers(4, 8, (13, E)))
            y[0] = np.where(own >= 0, own + N * rng.integers(0, 8 // N, E), y[0])
            x[q, g, :, V - E:] = 2 * y + rng.integers(0, 2, (16, E))
    return pack(x, kd, wt, th, rx, nx, tk)
def setup_inputs_spread(rng):
    x, kd, wt, th, rx, nx, tk = parts(rng)
    x = np.floor(np.exp2(4 * rng.random((N, 8, 1, V))) * rng.random(x.shape)).astype(np.int64)
    rx = np.floor(np.exp2(4 * rng.random((N, 8, 1, T))) * rng.random(rx.shape)).astype(np.int64)
    nx = np.floor(np.exp2(4 * rng.random((N, 8, 1, J, T))) * rng.random(nx.shape)).astype(np.int64)
    wt = np.floor(np.exp2(8 * rng.random(wt.shape)) * rng.random(wt.shape)).astype(np.int64); wt[..., 0] |= 1
    th = np.where(rng.random((N, 8)) < 0.25, rng.integers(0, 242, (N, 8)), rng.integers(20, 80, (N, 8)))
    kd = np.where(rng.random(kd.shape) < 0.2, A, np.floor(V * rng.random(kd.shape) ** 3).astype(np.int64))
    tk = codes(rng, 1 + np.floor(V * rng.random((N, 8, 16, T)) ** 3).astype(np.int64))
    return pack(x, kd, wt, th, rx, nx, tk)
def check_inputs(d):
    bad = []
    for k in ("x0", "rx", "nx"):
        a = d[k].astype(np.float32)
        if not np.all((a >= 0) & (a <= 15) & (a == np.floor(a))): bad.append("range of " + k)
    for k in ("k0", "k1"):
        a = d[k]
        if not np.all(((a >= 0) & (a < V)) | (a == A)): bad.append("range of " + k)
    if np.min(d["wt"]) < 0 or np.max(d["wt"]) > 255: bad.append("range of wt")
    if np.min(d["th"]) < 0 or np.max(d["th"]) > 241: bad.append("range of th")
    a = d["th"].reshape(-1, 8, 16)
    if not np.all(a == a[:, :, :1]): bad.append("th alike in a group")
    a = d["tk"].reshape(-1, 8, 16, T)
    if np.min(a[:, :, :F]) < 0 or np.max(a[:, :, :F]) > J + V: bad.append("kid codes of tk")
    if np.min(a[:, :, F]) < 1 or np.max(a[:, :, F]) > J: bad.append("feet of tk")
    if np.any(a[:, :, F + 1:] != 0): bad.append("unused rows of tk")
    return bad
def pick(a, ix):
    return np.take_along_axis(a, ix[:, None, :], 2)
def sweep(x, kd, S):
    a, b = kd[:, 0, :S], kd[:, 1, :S]
    m = np.maximum(pick(x, a), pick(x, b))
    for u in (a, b):
        for i in range(2):
            m = np.maximum(m, pick(x, pick(kd[:, i:i + 1], u)[:, 0]) - 2)
    x[:, :, :S] = (x[:, :, :S] + m) >> 1
def whole_of(a):
    return a.astype(np.float32).astype(np.int64)
def reference(x0, k0, k1, wt, th, rx, nx, tk):
    X = np.zeros((N, 8, 16, A + 1), np.int64); X[..., :V] = whole_of(x0).reshape(N, 8, 16, V)
    K = np.full((N, 8, 2, A + 1), A, np.int64)
    for q in range(N):
        K[q, :, 0, :V] = gentries(k0[q]); K[q, :, 1, :V] = gentries(k1[q])
    ws = wt.astype(np.int64).reshape(N, 8, 16, 1); lim = th.astype(np.int64).reshape(N, 8, 16)[:, :, :1]
    rt = whole_of(rx).reshape(N, 8, 16, T); nd = whole_of(nx).reshape(N, 8, 16, J, T); rec = tk.astype(np.int64).reshape(N, 8, 16, T)
    roots = np.ascontiguousarray(rt.transpose(1, 2, 3, 0)).reshape(8, 16, T * N)
    live = np.ones((N, 8, E), bool)
    for t in range(RO):
        S = V + E * t; fresh = np.zeros((N, 8, E), bool)
        for q in range(N):
            sweep(X[q], K[q], S)
            x = X[q][:, :, S - E:S].copy(); h = np.add.reduce(ws[q] * x, axis=1)
            took = np.full((8, E), -1, np.int64)
            for m in range(M):
                c = (h + 97 * m + 31 * t) & (T * N - 1)
                dist = np.add.reduce(np.abs(x - pick(roots, c)), axis=1)
                took = np.where((took < 0) & live[q] & (dist < lim[q]), c, took)
            for g in range(8):
                xg, kg = X[q, g], K[q, g]
                for o in range(N):
                    i = np.flatnonzero((took[g] >= 0) & ((took[g] & (N - 1)) == o))[:CAP]
                    if len(i) == 0: continue
                    s = took[g, i] >> LN; v = S - E + i; k = CAP * o + np.arange(len(i)); b = S + J * k
                    oldx = xg[:, v].copy(); oldk = kg[:, v].copy(); cd = rec[o, g][:, s]
                    back = v - (cd - J); back = np.where(back < 0, back + S, back)
                    new = np.where(cd == 0, A, np.where(cd <= J, b + cd - 1, back))
                    for j in range(1, J + 1):
                        foot = cd[F] == j
                        xg[:, b + j - 1] = np.where(foot, oldx, nd[o, g, :, j - 1][:, s])
                        kg[:, b + j - 1] = np.where(foot, oldk, new[2 * j:2 * j + 2])
                        fresh[q, g, J * k + j - 1] = True
                    kg[:, v] = new[0:2]
                    xg[:, v] = (oldx + rt[o, g][:, s]) >> 1
        live = fresh
    for q in range(N): sweep(X[q], K[q], A)
    return {"y": np.ascontiguousarray(X[..., :A]).reshape(N, 128, A).astype(np.float32).astype(BF)}

@@ -1,0 +1,764 @@
+from concourse.bass import DstId, RemoteDMATransfer
+from concourse.mybir import AluOpType, ActivationFunctionType
+
+AL = AluOpType
+AF = ActivationFunctionType
+V0, NT, E, A, RO = 1536, 256, 768, 3072, 2
+O = 16
+UP = 192.0
+CR = 12582912.0
+HALF = 63.0 / 128.0
+MW = 160
+MATS = ["I", "nI", "Ih", "I16", "I256", "I4k", "I64k", "I1m", "Iq", "nIq", "nI4k", "B1", "BW", "B14", "B0r", "B1r", "BO", "BO14",
+        "BOn", "BO6", "IW0", "IW1", "D01", "A1", "A2", "UN", "L0", "L1",
+        "K0", "K1", "K0a", "K0b", "K0c", "K0d", "K1a", "K1b", "K1c", "K1d"]
+BF, H16, F32, I32, U16 = "bfloat16", "float16", "float32", "int32", "uint16"
+SB = {
+    "X": (O + A, BF), "P": (O + A, BF), "RT": (2064, BF), "NTB": (2056, F32), "QT": (2056, F32),
+    "NX": (1536, BF), "TK": (256, I32), "KIN": (192, I32), "WT": (4, I32), "TH": (4, I32), "WB": (8, BF),
+    "KM": (384, F32), "LK": (384, U16), "KA": (192, F32), "KB": (192, F32),
+    "MAT": (MW * len(MATS), BF), "CC": (40, F32), "CI": (8, I32), "IO": (146, BF), "IOA": (128, BF), "IOB": (128, BF),
+    "KI": (128, BF), "VT": (392, F32), "DC": (48, F32), "M49": (392, BF), "D49": (392, H16),
+    "CZ": (256, H16), "CF": (8, H16), "UT": (128, BF), "UU": (128, BF),
+    "DD": (256, H16), "CQ": (256, BF), "P0": (256, BF), "PF": (256, F32),
+    "TA": (2048, BF), "TB": (3072, BF), "TC": (3072, BF), "TR": (3072, BF), "TD": (2048, BF), "TE": (2048, BF),
+    "HM": (144, I32), "HC": (144, I32), "HD": (144, I32), "PO": (144, I32), "CL": (144, U16),
+    "DF": (2304, BF), "AB": (2304, BF), "NR": (144, F32), "SC": (144, F32), "M01": (48, F32),
+    "MX": (48, I32), "KEY": (48, I32), "KEYB": (48, BF), "CT": (56, I32), "IB": (392, BF), "S1": (392, BF),
+    "LE": (392, BF), "S2": (392, H16), "RM": (392, BF), "L1": (8, U16), "L2F": (8, F32), "L2": (8, U16),
+    "EE": (128, BF), "CV": (256, H16), "KE": (256, H16), "SL": (16, U16), "FL": (8, U16),
+    "Z0": (128, BF), "OX": (128, BF), "RG": (128, BF), "XN": (128, BF), "G": (128, I32), "U": (768, I32),
+    "VR": (128, F32), "TT": (128, F32), "N1": (128, F32), "N2": (128, H16),
+    "OV": (48, BF), "NG": (96, F32), "LS": (48, U16), "KP": (96, H16), "WR": (192, F32), "DEAD": (48, BF),
+    "WW": (2048, BF), "ONE": (512, BF), "HI": (128, BF), "NB": (136, BF), "RB": (768, BF),
+}
+SCRATCH = {name: ("sbuf", [128, n], dtype) for name, (n, dtype) in SB.items()}
+for _b in range(8):
+    SCRATCH["ps%d" % _b] = ("psum", [128, 512], F32)
+WIDTH = {BF: 2, H16: 2, U16: 2, F32: 4, I32: 4}
+NDMA = 24
+SEMAPHORES = ["sv", "ss", "sp", "sg", "rt_in", "tab_in", "hand_in", "sent"] + ["d%d" % i for i in range(NDMA)]
+ESEM = {"v": "sv", "s": "ss", "p": "sp", "g": "sg"}
+
+COST = {"cyc": 1.04, "gat": 1.55, "sca": 3.8, "pe": 0.55, "vfix": 15.0, "sfix": 40.0, "hop": 120.0, "same": 60.0,
+        "rt_lat": 7000.0, "tab_lat": 11000.0, "dma": 1800.0, "rate": 250.0}
+PLAN = {
+    "first": [(128, "v"), (256, "v"), (384, "v"), (384, "v"), (256, "v"), (128, "v")],
+    "new": [[(192, "w"), (192, "w"), (192, "w"), (192, "w")], [(192, "w"), (192, "O"), (192, "w"), (192, "w")]],
+    "rest": [[(256, "v"), (256, "s"), (256, "v")], [(256, "m"), (256, "s"), (256, "w"), (256, "m"), (256, "w"), (256, "m")]],
+    "early": [[(256, "v")] * 3, [(256, "v")] * 6],
+    "late": [[(128, "v"), (256, "v"), (384, "v"), (256, "v"), (256, "v"), (256, "v")], [(384, "v")] * 4],
+    "last": [(384, "v"), (384, "o"), (384, "v"), (384, "v"), (384, "v"), (384, "o"), (384, "v"), (256, "v"), (128, "v")],
+    "dist": ["svsvvv", "vvsvvv"],
+    "patience": 300.0, "near": 0.5, "scalar": "ib",
+}
+
+
+def R(name, a, b, step=1):
+    return (name, a, b, step)
+
+
+def W(name):
+    return (name, 0, SCRATCH[name][1][1], 1)
+
+
+def IND(win, off):
+    return ("@", win, off)
+
+
+def M(name, a=0, n=128):
+    k = MATS.index(name) * MW
+    return ("MAT", k + a, k + a + n, 1)
+
+
+def KL(name, b, u, w):
+    k = 96 * (u // E) + 48 * b + (u % E) // 16
+    return (name, k, k + (w - u) // 16, 1)
+
+
+def ncols(r):
+    if r[0] == "@":
+        return 16 * ncols(r[2])
+    return (r[2] - r[1] + r[3] - 1) // r[3]
+
+
+def regs(r):
+    if not isinstance(r, tuple):
+        return []
+    if r[0] == "@":
+        return [r[1], r[2]]
+    return [r]
+
+
+def two_bytes(rs):
+    return all(WIDTH[SCRATCH[r[0]][2]] == 2 for r in rs)
+
+
+def build(rank, C, plan):
+    ops = []
+
+    def add(eng, kind, args, out, ins, cost, **kw):
+        rd, wr = [], []
+        for r in ins:
+            rd += regs(r)
+        for r in out:
+            if r[0] == "@":
+                wr.append(r[1]); rd.append(r[2])
+            else:
+                wr.append(r)
+        d = {"eng": eng, "kind": kind, "args": args, "rd": rd, "wr": wr, "cost": cost, "lat": 0.0, "at": 0.0}
+        d.update(kw)
+        ops.append(d)
+
+    def vcost(out, in0, full):
+        n = ncols(out)
+        if out[0] == "@":
+            return 50.0 + n * C["sca"] * C["cyc"]
+        if in0[0] == "@":
+            return 50.0 + n * C["gat"] * C["cyc"]
+        return C["vfix"] + max(64.0, n * full) * C["cyc"]
+
+    def ts(out, in0, s1, op0, s2=None, op1=None):
+        f = 0.5 if in0[0] != "@" and two_bytes([out, in0]) else 1.0
+        add("v", "ts", (out, in0, s1, s2, op0, op1), [out], [in0, s1, s2], vcost(out, in0, f))
+
+    def tt(out, in0, in1, op):
+        f = 1.0 if in0[0].startswith("ps") or in1[0].startswith("ps") else 2.0
+        add("v", "tt", (out, in0, in1, op), [out], [in0, in1], vcost(out, in0, f))
+
+    def cp(out, in0):
+        f = 0.5 if in0[0] != "@" and out[0] != "@" and two_bytes([out, in0]) else 1.0
+        add("v", "cp", (out, in0), [out], [in0], vcost(out, in0, f))
+
+    def scan(out, d0, d1, op0, op1):
+        f = 0.5 if two_bytes([out, d0, d1]) else 1.0
+        add("v", "scan", (out, d0, d1, 0.0, op0, op1), [out], [d0, d1], vcost(out, d0, f))
+
+    def ms(out, val):
+        add("v", "ms", (out, val), [out], [], vcost(out, out, 0.5 if two_bytes([out]) else 1.0))
+
+    def act(out, in0, func, bias=0.0, scale=1.0):
+        c = 65.0 + ncols(out) * C["gat"] * C["cyc"] if in0[0] == "@" else C["sfix"] + max(64, ncols(out)) * C["cyc"]
+        add("s", "act", (out, in0, func, bias, scale), [out], [in0, bias, scale], c)
+
+    def mm(out, pairs, start=True, stop=True):
+        ins = []
+        for l, r in pairs:
+            ins += [l, r]
+        add("p", "mm", (out, pairs, start, stop), [out], ins, 30.0 + len(pairs) * max(64, ncols(out)) * C["pe"])
+
+    def iota(out, pattern, base, mult=0):
+        add("g", "iota", (out, pattern, base, mult), [out], [], 130.0 + 2 * ncols(out) * C["cyc"])
+
+    def fill(out, val):
+        iota(out, [[0, ncols(out)]], val)
+
+    def aff(out, in0, scale, bias):
+        if "c" in plan["scalar"]:
+            act(out, in0, AF.Identity, bias, scale)
+        else:
+            ts(out, in0, scale, AL.mult, bias, AL.add)
+
+    def mat(kind, name, n, src, col, base, scale):
+        if kind in plan["scalar"]:
+            act(M(name, 0, n), M(base, 0, n), AF.Copy, 0.0, scale)
+        else:
+            ts(M(name, 0, n), src, col, AL.is_equal, scale, AL.mult)
+
+    nd = [0, 0]
+
+    def dma(q, kind, sb, dr, nbytes):
+        nd[1] = nd[1] + nbytes if kind == "load" else nbytes
+        add(q, kind, (sb, dr), [sb] if kind == "load" else [], [] if kind == "load" else [sb], 60.0,
+            lat=C["dma"] + nd[1] / C["rate"], sem="d%d" % nd[0])
+        nd[0] += 1
+
+    own = rank * NT
+    cc = lambda j: R("CC", j, j + 1)
+    dma("s", "load", R("KIN", 0, 96), ("k0",), 49152)
+    dma("s", "load", R("KIN", 96, 192), ("k1",), 49152)
+    dma("s", "load", R("RT", own, own + NT), ("rx",), 65536)
+    dma("y", "load", R("X", O, O + V0), ("x0",), 393216)
+    dma("y", "load", W("TK"), ("tk",), 131072)
+    dma("y", "load", W("NX"), ("nx",), 393216)
+    dma("y", "load", R("WT", 0, 1), ("wt",), 8192)
+    dma("y", "load", R("TH", 0, 1), ("th",), 8192)
+    iota(R("CI", 0, 1), [[0, 1]], 0, 1)
+    iota(W("IO"), [[1, 146]], 0)
+    iota(W("IOA"), [[16, 8], [0, 16]], 0)
+    iota(W("IOB"), [[16, 8], [0, 8], [128, 2]], 0)
+    add("g", "send", ("RT",), [], [R("RT", own, own + NT)], 1500.0, lat=C["rt_lat"])
+    for o in range(8):
+        if o != rank:
+            add("x", "arrive", ("rt_in",), [R("RT", o * NT, o * NT + NT)], [], 0.0, sem="rt_in")
+            add("x", "arrive", ("tab_in",), [R("NTB", o * NT, o * NT + NT), R("QT", o * NT, o * NT + NT)], [], 0.0, sem="tab_in")
+    ms(R("X", 0, O), 0.0); ms(R("P", 0, O), 0.0)
+    ts(W("KA"), W("KIN"), -1024.0, AL.add)
+    ts(W("KB"), W("KIN"), -8.0, AL.mult, 20480.0, AL.add)
+    for j in range(2):
+        for b in range(2):
+            k = 96 * b + 48 * j
+            tt(KL("KM", b, E * j, E * j + E), R("KA", k, k + 48), R("KB", k, k + 48), AL.min)
+        ts(R("LK", 96 * j, 96 * j + 96), R("KM", 96 * j, 96 * j + 96), 1024.25 + O, AL.add)
+    ts(R("CI", 1, 2), R("CI", 0, 1), 15, AL.bitwise_and)
+    ts(R("CI", 2, 3), R("CI", 0, 1), 1, AL.logical_shift_right, 7, AL.bitwise_and)
+    ts(R("CI", 3, 4), R("CI", 0, 1), 1, AL.bitwise_and)
+    cp(R("CC", 0, 4), R("CI", 0, 4))
+    io = R("IO", 0, 128)
+    ts(M("I"), io, cc(0), AL.is_equal)
+    for nm, sc in (("nI", -1.0), ("Ih", HALF), ("IW0", UP - 1.0), ("IW1", 2.0), ("I16", 16.0), ("I256", 256.0), ("I4k", 4096.0),
+                   ("I64k", 65536.0), ("I1m", 1048576.0), ("Iq", 1.0 / 2048.0), ("nIq", -1.0 / 2048.0), ("nI4k", -4096.0)):
+        mat("i", nm, 128, io, cc(0), "I", sc)
+    tt(cc(4), cc(0), cc(1), AL.subtract)
+    aff(cc(5), cc(4), 1.0, 15.0)
+    aff(cc(7), cc(2), 1.0, -16.0)
+    ts(cc(8), cc(1), 14.0, AL.is_equal)
+    io3 = R("IO", 0, 143)
+    ts(M("B1", 0, 143), io3, cc(5), AL.is_equal)
+    mat("b", "B14", 143, io3, cc(5), "B1", cc(8))
+    ts(M("BO"), W("IOA"), cc(4), AL.is_equal)
+    mat("b", "BO14", 128, W("IOA"), cc(4), "BO", cc(8))
+    mat("b", "BOn", 128, W("IOA"), cc(4), "BO", -16384.0)
+    mat("b", "BO6", 128, W("IOA"), cc(4), "BO", 6.0)
+    ts(W("CQ"), W("TK"), 6.0, AL.min, -16.0, AL.add)
+    ts(W("DD"), W("TK"), -6.0, AL.add, 0.0, AL.max)
+    ts(W("P0"), W("TK"), 0.0, AL.is_equal, -8192.0, AL.mult)
+    mm(R("ps6", 0, NT), [(M("BO14"), W("CQ"))])
+    mm(R("ps7", 0, NT), [(M("Iq"), W("CQ")), (M("nI"), W("DD")), (M("I"), W("P0"))])
+    ts(W("PF"), R("ps6", 0, NT), cc(7), AL.is_equal, -16384.0, AL.mult)
+    tt(R("QT", own, own + NT), R("ps7", 0, NT), W("PF"), AL.min)
+    mm(R("ps5", 0, NT), [(M(n), R("NX", w * NT, w * NT + NT)) for w, n in enumerate(("I", "I16", "I256", "I4k", "I64k", "I1m"))])
+    act(R("NTB", own, own + NT), R("ps5", 0, NT), AF.Copy)
+    add("g", "send", ("NTB",), [], [R("NTB", own, own + NT)], 1000.0, lat=C["tab_lat"])
+    add("g", "send", ("QT",), [], [R("QT", own, own + NT)], 1000.0, lat=C["tab_lat"])
+    cp(cc(9), R("WT", 0, 1)); cp(cc(10), R("TH", 0, 1)); cp(R("WB", 0, 1), R("WT", 0, 1))
+    mat("b", "BW", 143, io3, cc(5), "B1", cc(9))
+    mm(R("ps6", 0, 1), [(M("BO"), R("WB", 0, 1))])
+    act(cc(24), R("ps6", 0, 1), AF.Copy, 0.0, -UP)
+    ts(W("UT"), io, cc(0), AL.is_lt, -1.0, AL.mult)
+    ts(W("UU"), io, cc(0), AL.is_equal, 1024.0, AL.mult)
+    tt(W("UT"), W("UT"), W("UU"), AL.add)
+    tt(M("UN"), W("UT"), M("BO"), AL.mult)
+    fill(R("RT", 2048, 2064), 0)
+    fill(W("M49"), 1); fill(R("M49", 0, 392, 49), 0); fill(R("IB", 48, 392, 49), 1)
+    iota(W("KI"), [[0, 8], [1, 16]], 1)
+    iota(W("VT"), [[0, 8], [16, 49]], 0)
+    fill(R("CT", 48, 56), 2048); fill(R("NTB", 2048, 2056), 0); fill(R("KM", 192, 384), 0)
+    for j in range(4):
+        fill(R("X", O + V0 + 384 * j, O + V0 + 384 * j + 384), int(UP))
+    iota(W("DC"), [[0, 8], [16, 6]], 0)
+    act(R("QT", 2048, 2056), R("IO", 0, 8), AF.Identity, cc(8), 0.0)
+    act(R("QT", 2048, 2056), R("QT", 2048, 2056), AF.Identity, -8192.0, 8192.0 - 14.0 / 2048.0)
+    aff(cc(6), cc(4), 1.0, 128.0)
+    aff(cc(11), cc(1), 6.0, 0.0)
+    aff(cc(12), cc(1), -6.0, 858.0)
+    aff(cc(25), cc(1), 1.0, 0.5)
+    ts(M("L0"), W("IOB"), cc(4), AL.is_equal)
+    ts(M("L1"), W("IOB"), cc(6), AL.is_equal)
+    act(W("VT"), W("VT"), AF.Identity, cc(1), 1.0)
+    act(R("VT", 48, 392, 49), R("IO", 0, 8), AF.Identity, cc(12), 96.0)
+    act(W("DC"), W("DC"), AF.Identity, cc(1), 1.0)
+    ts(W("D49"), W("M49"), 0.0, AL.mult)
+    ts(R("D49", 0, 392, 49), R("IO", 0, 8), 98.0, AL.mult, 48.0, AL.add)
+    for t in range(RO):
+        ts(R("CZ", 128 * t, 128 * t + 128), io, 6.0, AL.mult, float(V0 + E * t - 1024), AL.add)
+    ts(W("CF"), R("IO", 0, 8), 96.0, AL.mult, cc(11), AL.add)
+    ts(cc(13), cc(2), 1.0, AL.max, 6.0, AL.min)
+    aff(cc(14), cc(2), 501.0, cc(5))
+    aff(cc(15), cc(13), -500.0, cc(14))
+    aff(cc(16), cc(3), 1000.0, -2.0)
+    aff(cc(17), cc(3), -1000.0, 998.0)
+    aff(cc(26), cc(16), 1.0, cc(15))
+    aff(cc(27), cc(17), 1.0, cc(15))
+    for j, (val, op) in enumerate(((9.5, AL.is_lt), (9.5, AL.is_gt), (5.5, AL.is_lt), (5.5, AL.is_gt))):
+        ts(cc(18 + j), cc(1), val, op)
+    ts(cc(28), cc(1), 3.5, AL.is_lt)
+    ts(cc(23), cc(28), cc(3), AL.mult)
+    aff(cc(22), cc(23), -1.0, cc(28))
+    fill(W("ONE"), 1)
+    fill(R("NB", 0, 8), 0)
+    ts(cc(29), cc(1), 1.5, AL.is_lt)
+    ts(cc(30), cc(29), 2.0, AL.mult, cc(28), AL.subtract)
+    aff(cc(31), cc(0), 1.0, 2.0)
+    mat("i", "D01", 128, io, cc(0), "I", cc(29))
+    mat("i", "A2", 128, io, cc(0), "I", cc(30))
+    ts(M("A1"), io, cc(31), AL.is_equal, cc(29), AL.mult)
+    for b in range(2):
+        ts(M("K%d" % b, 0, 146), W("IO"), cc(26 + b), AL.is_equal)
+        for j, x in enumerate("abcd"):
+            mat("k", "K%d%s" % (b, x), 146, W("IO"), cc(26 + b), "K%d" % b, cc(18 + j))
+        mat("b", "B%dr" % b, 143, io3, cc(5), "B1", cc(22 + b))
+
+    rot = {}
+
+    def nxt(k, n):
+        rot[k] = (rot.get(k, 0) + 1) % n
+        return rot[k]
+
+    def bank():
+        return "ps%d" % (5 + nxt("m", 3))
+
+    def tmp(name, n):
+        k = 512 * nxt(name, SB[name][0] // 512)
+        return R(name, k, k + n)
+
+    def stage1(u, S, pieces):
+        for n, how in pieces:
+            w = u + n
+            ta, pp = tmp("TA", n), R("P", O + u, O + w)
+            g0, g1 = (IND(R("X", 0, O + S), KL("LK", b, u, w)) for b in range(2))
+            if how == "o":
+                cp(ta, g0)
+            else:
+                act(ta, g0, AF.Copy)
+            if how != "s":
+                tt(pp, g1, ta, AL.max)
+            else:
+                td, te = tmp("TD", n), tmp("TE", n)
+                pd = R("ps%d" % (3 + nxt("d", 2)), 0, n); pa = R("ps%d" % nxt("a", 3), 0, n)
+                act(td, g1, AF.Copy)
+                mm(pd, [(M("nI"), ta), (M("I"), td)])
+                act(te, pd, AF.Relu)
+                mm(pa, [(M("I"), ta), (M("I"), te)])
+                act(pp, pa, AF.Copy)
+            u = w
+
+    def stage2(u, S, pieces, sweep):
+        for n, how in pieces:
+            w = u + n
+            tb, tc, tr = tmp("TB", n), tmp("TC", n), tmp("TR", n)
+            if sweep == RO:
+                pa = R("ps%d" % (0, 1, 2, 5, 6)[nxt("a5", 5)], 0, n); pd = R("ps%d" % (3, 4, 7)[nxt("d3", 3)], 0, n)
+            else:
+                pa = R("ps%d" % nxt("a", 3), 0, n); pd = R("ps%d" % (3 + nxt("d", 2)), 0, n)
+            xs, pp = R("X", O + u, O + w), R("P", O + u, O + w)
+            g0, g1 = (IND(R("P", 0, O + S), KL("LK", b, u, w)) for b in range(2))
+            lift = UP if sweep == 0 else UP - 2 * UP * HALF
+            if how in "oO":
+                cp(tb, g0)
+            else:
+                act(tb, g0, AF.Copy)
+            if how in "wO":
+                ww = tmp("WW", n)
+                mm(pd, [(M("Ih"), xs), (M("Ih"), pp)])
+                act(ww, pd, AF.Identity, lift, 1.0)
+                mm(pa, [(M("IW%d" % sweep), R("ONE", 0, n)), (M("Ih"), xs)], True, False)
+                tt(tc, g1, tb, AL.max)
+                mm(pa, [(M("Ih"), tc)], False, True)
+                tt(xs, pa, ww, AL.max)
+                u = w
+                continue
+            mm(pa, [(M("Ih"), xs), (M("Ih"), pp)], True, False)
+            if how == "s":
+                te = tmp("TE", n)
+                act(tc, g1, AF.Copy)
+                mm(pd, [(M("nI"), tb), (M("I"), tc)])
+                act(te, pd, AF.Relu)
+                mm(pd, [(M("nI"), pp), (M("I"), tb), (M("I"), te)])
+            else:
+                tt(tc, g1, tb, AL.max)
+                mm(pd, [(M("nI"), pp), (M("I"), tc)])
+            act(tr, pd, AF.Relu, -2.0, 1.0)
+            mm(pa, [(M("Ih"), tr)], False, True)
+            if sweep == RO:
+                ts(xs, pa, CR, AL.add, -CR - 2 * UP * HALF, AL.add)
+                dma("y", "store", xs, ("y", u, w), 256 * n)
+            elif how in "vo":
+                ts(xs, pa, lift, AL.add)
+            else:
+                act(xs, pa, AF.Identity, lift, 1.0)
+            u = w
+
+    def sel(base, src, a, n):
+        return [(M(base, 15 - r), R(src, a + r, a + n, 16)) for r in range(16)]
+
+    stage1(0, V0, plan["first"])
+    fill(R("X", 0, O), int(UP))
+    for t in range(RO):
+        S = V0 + E * t
+        nw = O + S - E
+        kc = 96 * (t + 1)
+        stage2(S - E, S, plan["new"][t], t)
+        pb = bank()
+        mm(R(pb, 0, 48), sel("BW", "X", nw, E))
+        for m in range(3):
+            ts(R("HM", 48 * m, 48 * m + 48), R(pb, 0, 48), cc(24), AL.add, float(97 * m + 31 * t), AL.add)
+        ts(W("HC"), W("HM"), 2047, AL.bitwise_and)
+        ts(W("HD"), W("HC"), 2049.0, AL.mult)
+        ts(W("PO"), W("HD"), 3, AL.logical_shift_right, 2047, AL.bitwise_and)
+        cp(W("CL"), W("PO"))
+        for m in range(3):
+            for h in range(2):
+                a = E * m + 384 * h
+                gr = IND(W("RT"), R("CL", 48 * m + 24 * h, 48 * m + 24 * h + 24))
+                xs, df, ab = R("X", nw + 384 * h, nw + 384 * h + 384), R("DF", a, a + 384), R("AB", a, a + 384)
+                if plan["dist"][t][2 * m + h] == "v":
+                    tt(df, gr, xs, AL.subtract)
+                    act(ab, df, AF.Abs, UP, 1.0)
+                else:
+                    pd = R("ps%d" % (3 + nxt("d", 2)), 0, 384)
+                    act(df, gr, AF.Copy)
+                    mm(pd, [(M("nI"), xs), (M("I"), df)])
+                    act(ab, pd, AF.Abs, UP, 1.0)
+            pb = bank()
+            mm(R(pb, 0, 48), ([(M("I256"), W("DEAD"))] if t else []) + sel("B1", "AB", E * m, E))
+            nr, sc = R("NR", 48 * m, 48 * m + 48), R("SC", 48 * m, 48 * m + 48)
+            ts(nr, R(pb, 0, 48), cc(10), AL.is_lt, 2048.0 * (5 - 2 * m), AL.mult)
+            tt(sc, nr, R("PO", 48 * m, 48 * m + 48), AL.add)
+            if m == 1:
+                tt(W("M01"), R("SC", 0, 48), R("SC", 48, 96), AL.max)
+        tt(W("MX"), W("M01"), R("SC", 96, 144), AL.max)
+        ts(W("KEY"), W("MX"), 8, AL.logical_shift_right, 15, AL.bitwise_and)
+        for o in range(8):
+            ts(R("IB", 49 * o, 49 * o + 48), W("KEY"), float(8 + o), AL.is_equal)
+        scan(W("S1"), W("M49"), W("IB"), AL.mult, AL.add)
+        ts(R("CT", 0, 48), W("MX"), 2047, AL.bitwise_and)
+        cp(W("KEYB"), W("KEY"))
+        p1, p2 = bank(), bank()
+        mm(R(p1, 0, 392), [(M("BO"), W("S1"))])
+        mm(R(p2, 0, 392), [(M("UN"), W("IB")), (M("BO"), W("S1"))])
+        act(W("LE"), R(p1, 0, 392), AF.Sign, cc(25), -1.0)
+        act(W("RM"), R(p2, 0, 392), AF.Relu, -1024.0, 1.0)
+        scan(W("S2"), W("D49"), W("LE"), AL.max, AL.add)
+        s2 = R("S2", 47, 392, 49)
+        ts(W("L1"), s2, 0.5, AL.mult, 0.25, AL.add)
+        tt(W("EE"), IND(W("RM"), W("L1")), W("KI"), AL.is_equal)
+        tt(W("L2F"), s2, R("D49", 0, 392, 49), AL.subtract)
+        ts(W("L2"), W("L2F"), 0.5, AL.mult, 24.25, AL.add)
+        tt(R("CV", 128, 256), IND(W("VT"), W("L1")), W("EE"), AL.mult)
+        tt(R("CV", 0, 128), IND(W("CT"), W("L2")), W("EE"), AL.mult)
+        pb = bank()
+        mm(R(pb, 0, 16), sel("B1", "CV", 0, 256))
+        ts(W("SL"), R(pb, 0, 16), 0.25, AL.add)
+        cl, vl = R("SL", 0, 8), R("SL", 8, 16)
+        pv = bank()
+        mm(R(pv, 0, 128), [(M("BO"), R("CV", 128, 256))])
+        act(W("VR"), R(pv, 0, 128), AF.Identity, float(S - E - 1024), 1.0)
+        for b in range(2):
+            tt(R("KE", 128 * b, 128 * b + 128), IND(R("KM", kc + 48 * b, kc + 48 * b + 56), W("L2")), W("EE"), AL.mult)
+        pr = bank()
+        rm = [(M("I"), R("RM", 49 * o, 49 * o + 48)) for o in range(8)]
+        mm(R(pr, 0, 48), rm)
+        act(W("OV"), R(pr, 0, 48), AF.Relu, -16.0, 1.0)
+        for b in range(2):
+            mm(R(pr, 48 * b, 48 * b + 48), [(M("I16"), W("KEYB"))] + rm + [(M("nI4k"), W("OV"))])
+        ts(W("LS"), R(pr, 0, 48), -129.0 + 8.25, AL.add)
+        ts(W("NG"), R(pr, 0, 96), 128.5, AL.is_lt)
+        tt(W("KP"), R("KM", kc, kc + 96), W("NG"), AL.mult)
+        if t + 1 < RO:
+            pb = bank()
+            for c6 in range(6):
+                mm(R(pb, c6, 48, 6), [(M("BO6"), R("S1", 47, 392, 49))])
+            tt(W("DEAD"), R(pb, 0, 48), W("DC"), AL.is_le)
+        act(W("Z0"), IND(W("QT"), cl), AF.Identity, 15.0, 2048.0)
+        tt(W("TT"), IND(W("QT"), cl), W("VR"), AL.add)
+        pz, pu = bank(), bank()
+        mm(R(pz, 0, 128), [(M("I"), R("CZ", 128 * t, 128 * t + 128)), (M("I"), W("Z0"))])
+        mm(R(pu, 0, 128), [(M("BOn"), W("EE")), (M("L0"), R("KE", 0, 128)), (M("L1"), R("KE", 128, 256)), (M("nIq"), W("Z0"))])
+        tt(W("N1"), R(pz, 0, 128), W("TT"), AL.max)
+        tt(W("N2"), R(pu, 0, 128), W("N1"), AL.max)
+        xw = R("X", nw, nw + 2 * E)
+        act(W("OX"), IND(xw, vl), AF.Copy)
+        act(W("RG"), IND(W("RT"), cl), AF.Copy)
+        cp(W("G"), IND(W("NTB"), cl))
+        pb = bank()
+        mm(R(pb, 0, 128), [(M("Ih"), W("OX")), (M("Ih"), W("RG"))])
+        act(W("XN"), R(pb, 0, 128), AF.Identity, UP - UP * HALF, 1.0)
+        cp(IND(xw, vl), W("XN"))
+        pf = bank()
+        mm(R(pf, 0, 8), [(M("I"), W("CF"))] + sel("B14", "Z0", 0, 128))
+        ts(W("FL"), R(pf, 0, 8), 0.25, AL.add)
+        for w in range(6):
+            ts(R("U", w, E, 6), W("G"), 4 * w, AL.logical_shift_right, 15, AL.bitwise_and)
+        ts(R("X", O + S, O + S + E), W("U"), UP, AL.add)
+        cp(IND(R("X", O + S, O + S + E), W("FL")), W("OX"))
+
+        def finish(pb, col):
+            src, km, lk = R(pb, 0, 96), R("KM", col, col + 96), R("LK", col, col + 96)
+            if t == 0:
+                wr = R("WR", col - kc, col - kc + 96)
+                ts(wr, src, -1024.5, AL.is_lt, float(S), AL.mult)
+                tt(km, src, wr, AL.add)
+                src = km
+            ts(lk, src, 1024.25 + O, AL.add)
+
+        pn = bank()
+        for b in range(2):
+            for co, us in enumerate((((0, ""), (1, ""), (2, "a")), ((2, "b"), (3, ""), (4, ""), (5, "c")), ((5, "d"), (6, ""), (7, "")))):
+                mm(R(pn, 48 * b + co, 48 * b + 48, 3),
+                   [(M("K%d%s" % (b, x), 14 - (6 * u - 16 * co)), R("N2", u, 128, 8)) for u, x in us])
+        finish(pn, kc + 96)
+        p1, p2 = bank(), bank()
+        mm(R(p1, 0, 128), [(M("D01"), W("N2")), (M("A1"), W("N2"))])
+        act(W("HI"), R(p1, 0, 128), AF.Copy)
+        mm(R(p2, 0, 128), [(M("A1"), W("N2")), (M("A2"), W("HI"))])
+        act(R("NB", 8, 136), R(p2, 0, 128), AF.Copy)
+        act(W("RB"), IND(W("NB"), W("LS")), AF.Copy)
+        pk = bank()
+        for b in range(2):
+            mm(R(pk, 48 * b, 48 * b + 48), [(M("I"), R("KP", 48 * b, 48 * b + 48))] + sel("B%dr" % b, "RB", 0, E))
+        finish(pk, kc)
+        stage2(0, S, plan["rest"][t], t)
+        stage1(0, S, plan["early"][t])
+        stage1(S, S + E, plan["late"][t][:len(plan["late"][t]) // 2])
+        stage1(S - E, S + E, plan["late"][t][len(plan["late"][t]) // 2:])
+    stage2(0, A, plan["last"], RO)
+    return ops
+
+
+def depend(ops):
+    hist = {}
+    for n, op in enumerate(ops):
+        dep = {}
+        for kind, rs in (("r", op["rd"]), ("w", op["wr"])):
+            for r in rs:
+                ps = r[0].startswith("ps")
+                for k, kk, a, b in hist.get(r[0], []):
+                    if k == n:
+                        continue
+                    other = ops[k]
+                    same = other["eng"] == op["eng"] and "sem" not in other and "sem" not in op
+                    hit = a < r[2] and r[1] < b
+                    if ps and not same:
+                        dep[k] = True
+                    elif hit and (kind == "w" or kk == "w"):
+                        wait = (not same) or (kk == "w" and op["eng"] != "p")
+                        dep[k] = dep.get(k, False) or wait
+                    elif ps and op["eng"] == "p":
+                        dep[k] = dep.get(k, False)
+        for kind, rs in (("r", op["rd"]), ("w", op["wr"])):
+            for r in rs:
+                h = hist.setdefault(r[0], [])
+                if kind == "w" and r[3] == 1 and not r[0].startswith("ps"):
+                    h[:] = [e for e in h if not (r[1] <= e[2] and e[3] <= r[2])]
+                elif r[0].startswith("ps"):
+                    h[:] = h[-24:]
+                h.append((n, kind, r[1], r[2]))
+        op["dep"] = dep
+    last = {}
+    for n, op in enumerate(ops):
+        if op["kind"] in ("send", "load"):
+            if op["eng"] in last:
+                op["dep"].setdefault(last[op["eng"]], False)
+            last[op["eng"]] = n
+    for op in ops:
+        if op["kind"] == "arrive":
+            for n, o2 in enumerate(ops):
+                if o2["kind"] == "send" and (o2["args"][0] == "RT") == (op["sem"] == "rt_in"):
+                    op["dep"][n] = True
+
+
+def order(ops, C, plan):
+    n = len(ops)
+    kids = [[] for _ in range(n)]
+    for k, op in enumerate(ops):
+        for d in op["dep"]:
+            kids[d].append(k)
+    way = [-1.0] * n
+    todo = list(range(n - 1, -1, -1))
+    while todo:
+        rest = []
+        for k in todo:
+            if any(way[c] < 0 for c in kids[k]):
+                rest.append(k)
+            else:
+                op = ops[k]
+                way[k] = op["cost"] + max([way[c] + (op["lat"] + C["hop"] if ops[c]["dep"][k] else 0.0) for c in kids[k]] + [op["lat"]])
+        todo = rest
+    left = [len(op["dep"]) for op in ops]
+    ready = [op["at"] for op in ops]
+    free = {}
+    pool = {}
+    for k in range(n):
+        if left[k] == 0:
+            pool.setdefault(ops[k]["eng"], []).append(k)
+    seq = {}
+    end = 0.0
+    for _ in range(n):
+        best = None
+        for e, p in pool.items():
+            if not p:
+                continue
+            now = max(free.get(e, 0.0), min(ready[k] for k in p))
+            k = max((k for k in p if ready[k] <= now), key=lambda j: way[j])
+            for j in p:
+                if ready[j] > now and way[j] - way[k] > plan["patience"] and ready[j] - now < plan["near"] * ops[k]["cost"]:
+                    k = j
+            st = max(now, ready[k])
+            if best is None or st < best[0]:
+                best = (st, e, k)
+        st, e, k = best
+        pool[e].remove(k)
+        seq.setdefault(e, []).append(k)
+        free[e] = st + ops[k]["cost"]
+        ops[k]["st"] = st
+        if ops[k]["kind"] != "send":
+            end = max(end, free[e] + ops[k]["lat"])
+        for c in kids[k]:
+            if ops[c]["dep"][k]:
+                same = ops[c]["eng"] == e and "sem" not in ops[k]
+                ready[c] = max(ready[c], free[e] + ops[k]["lat"] + (C["same"] if same else C["hop"]))
+            else:
+                ready[c] = max(ready[c], free[e])
+            left[c] -= 1
+            if left[c] == 0:
+                pool.setdefault(ops[c]["eng"], []).append(c)
+    return seq, end
+
+
+def hands(T, topo, rank):
+    me = T.cores[rank]
+    others = sorted((c for c in topo.cores_of(me) if c != me), key=lambda c: (topo.die(c) == topo.die(me), c))
+    n = len(T.cores)
+    dst = [(rank + 1 + j) % n for j in range(n - 1)]
+    pairs = [("NTB", d) for d in dst] + [("QT", d) for d in reversed(dst)]
+    mix = [0, 4, 1, 5, 2, 6, 3]
+    return {others[mix[j]]: pairs[2 * j:2 * j + 2] for j in range(n - 1)}
+
+
+def bits(es):
+    m = 0
+    for e in es:
+        m |= 1 << e
+    return m
+
+
+def dst_id(topo, dst, src):
+    rid, pid = topo.addr(dst, src)
+    return DstId(rid=rid, pnc=pid)
+
+
+def helper(g, core, T, topo):
+    for rank, me in enumerate(T.cores):
+        if core in topo.cores_of(me):
+            pairs = hands(T, topo, rank)[core]
+            g.wait_ge(T.sem.hand_in, len(topo.engines(me, core)) * len(set(p[0] for p in pairs)))
+            trs = []
+            used = 0
+            for j, (name, d) in enumerate(pairs):
+                es = topo.engines(core, T.cores[d])
+                h = len(es) // 2
+                used += h
+                trs.append(RemoteDMATransfer(dst_ids=[dst_id(topo, T.cores[d], core)], dma_engine_mask=bits(es[j * h:j * h + h]),
+                                             remote_sem=T.sem.tab_in, src=T[name][:, 0:NT], dst=T[name][:, rank * NT:rank * NT + NT]))
+            g.remote_dma_fused(trs, local_sem=T.sem.sent)
+            g.wait_ge(T.sem.sent, used)
+
+
+def rank_program(g, core, T, topo):
+    rank = T.rank_of(core)
+    if rank is None:
+        helper(g, core, T, topo)
+        return
+    ops = build(rank, COST, PLAN)
+    depend(ops)
+    seq, _ = order(ops, COST, PLAN)
+    Q = {"v": g.vector, "s": g.scalar, "p": g.tensor, "g": g, "y": g.sync}
+    plan = hands(T, topo, rank)
+    peers = [c for c in T.cores if c != core]
+    off = topo.engines(core, peers[0])
+
+    def ap(r):
+        if not isinstance(r, tuple):
+            return r
+        if r[0] == "@":
+            return ap(r[1]).indirect(ap(r[2]))
+        return T[r[0]][:, r[1]:r[2]:r[3]] if r[3] != 1 else T[r[0]][:, r[1]:r[2]]
+
+    needed = set()
+    for op in ops:
+        for d, wait in op["dep"].items():
+            if wait:
+                needed.add(d)
+    count = {}
+    total = {}
+    for e, ks in seq.items():
+        if e in ESEM:
+            cs = [k for k in ks if "sem" not in ops[k] and ops[k]["kind"] != "send"]
+            needed.add(cs[-1])
+            c = 0
+            for k in cs:
+                if k in needed:
+                    c += 1
+                    count[k] = (ESEM[e], c)
+            total[ESEM[e]] = c
+    for k, op in enumerate(ops):
+        if op["kind"] == "arrive":
+            count[k] = (op["sem"], len(off) * len(peers))
+        elif "sem" in op:
+            count[k] = (op["sem"], 16)
+        if "sem" in op:
+            total[count[k][0]] = count[k][1]
+    sent = [0]
+
+    def send(name):
+        src = T[name][:, rank * NT:rank * NT + NT]
+        if name == "RT":
+            es = off
+            tr = RemoteDMATransfer(dst_ids=[dst_id(topo, c, core) for c in peers], dma_engine_mask=bits(es), remote_sem=T.sem.rt_in,
+                                   src=src, dsts=[src] * len(peers))
+        else:
+            to = [c for c, pairs in plan.items() if name in [p[0] for p in pairs]]
+            es = topo.engines(core, to[0])
+            tr = RemoteDMATransfer(dst_ids=[dst_id(topo, c, core) for c in to], dma_engine_mask=bits(es), remote_sem=T.sem.hand_in,
+                                   src=src, dsts=[T[name][:, 0:NT]] * len(to))
+        g.remote_dma_fused([tr], local_sem=T.sem.sent)
+        sent[0] += len(es)
+
+    for e, ks in seq.items():
+        if e == "x":
+            continue
+        q = Q[e]
+        seen = {}
+        for k in ks:
+            op = ops[k]
+            want = {}
+            for d, wait in op["dep"].items():
+                if wait:
+                    s, c = count[d]
+                    want[s] = max(want.get(s, 0), c)
+            for s, c in want.items():
+                if seen.get(s, 0) < c:
+                    q.wait_ge(T.sem[s], c)
+                    seen[s] = c
+            a = op["args"]
+            kind = op["kind"]
+            if kind == "send":
+                send(a[0])
+                continue
+            if kind == "load":
+                q.dma_start(ap(a[0]), T[a[1][0]][:]).then_inc(T.sem[op["sem"]], 16)
+                continue
+            if kind == "store":
+                q.dma_start(T.y[:, a[1][1]:a[1][2]], ap(a[0])).then_inc(T.sem[op["sem"]], 16)
+                continue
+            if kind == "ts":
+                if a[5] is None:
+                    ins = q.tensor_scalar(ap(a[0]), ap(a[1]), ap(a[2]), None, a[4])
+                else:
+                    ins = q.tensor_scalar(ap(a[0]), ap(a[1]), ap(a[2]), ap(a[3]), a[4], a[5])
+            elif kind == "tt":
+                ins = q.tensor_tensor(ap(a[0]), ap(a[1]), ap(a[2]), a[3])
+            elif kind == "cp":
+                ins = q.tensor_copy(ap(a[0]), ap(a[1]))
+            elif kind == "scan":
+                ins = q.tensor_tensor_scan(ap(a[0]), ap(a[1]), ap(a[2]), a[3], a[4], a[5])
+            elif kind == "ms":
+                ins = q.memset(ap(a[0]), a[1])
+            elif kind == "act":
+                if a[2] == AF.Copy:
+                    ins = q.activation(ap(a[0]), ap(a[1]), a[2], scale=ap(a[4]))
+                else:
+                    ins = q.activation(ap(a[0]), ap(a[1]), a[2], bias=ap(a[3]), scale=ap(a[4]))
+            elif kind == "mm":
+                for j, (l, r) in enumerate(a[1]):
+                    ins = q.matmul(ap(a[0]), ap(l), ap(r), a[2] and j == 0, a[3] and j == len(a[1]) - 1)
+            elif SCRATCH[a[0][0]][2] == I32:
+                ins = q.iota(ap(a[0]), a[1], a[2], a[3])
+            else:
+                ins = q.iota(ap(a[0]), a[1], a[2], a[3], allow_small_or_imprecise_dtypes=True)
+            if k in count:
+                ins.then_inc(T.sem[count[k][0]], 1)
+    g.wait_ge(T.sem.sent, sent[0])
+    for s, c in total.items():
+        g.sync.wait_ge(T.sem[s], c)

@@ -5,52 +5,60 @@ AL = AluOpType
 AF = ActivationFunctionType
 V0, NT, E, A, RO = 1536, 256, 768, 3072, 2
 O = 16
-UP = 192.0
+UP = 160.0
 CR = 12582912.0
-HALF = 63.0 / 128.0
+HALF = 31.0 / 64.0
 MW = 160
-MATS = ["I", "nI", "Ih", "I16", "I256", "I4k", "I64k", "I1m", "Iq", "nIq", "nI4k", "B1", "BW", "B14", "B0r", "B1r", "BO", "BO14",
-        "BOn", "BO6", "IW0", "IW1", "D01", "A1", "A2", "UN", "L0", "L1",
+MATS = ["I", "nI", "Ih", "I16", "I256", "I4k", "I64k", "I1m", "Iq", "nIq", "IB", "B1", "BW", "B0r", "B1r", "BO", "BO14",
+        "nBO", "nBO6", "nBOk", "DI", "IW0", "IW1", "nD", "A3", "nU", "L0", "L1",
         "K0", "K1", "K0a", "K0b", "K0c", "K0d", "K1a", "K1b", "K1c", "K1d"]
 BF, H16, F32, I32, U16 = "bfloat16", "float16", "float32", "int32", "uint16"
 SB = {
-    "X": (O + A, BF), "P": (O + A, BF), "RT": (2064, BF), "NTB": (2056, F32), "QT": (2056, F32),
-    "NX": (1536, BF), "TK": (256, I32), "KIN": (192, I32), "WT": (4, I32), "TH": (4, I32), "WB": (8, BF),
-    "KM": (384, F32), "LK": (384, U16), "KA": (192, F32), "KB": (192, F32),
-    "MAT": (MW * len(MATS), BF), "CC": (40, F32), "CI": (8, I32), "IO": (146, BF), "IOA": (128, BF), "IOB": (128, BF),
-    "KI": (128, BF), "VT": (392, F32), "DC": (48, F32), "M49": (392, BF), "D49": (392, H16),
-    "CZ": (256, H16), "CF": (8, H16), "UT": (128, BF), "UU": (128, BF),
+    "X": (O + A, BF), "P": (O + A, BF), "RT": (2064, BF), "QT": (2056, F32), "NTB": (2056, F32), "NX": (V0, BF),
+    "G": (128, I32), "U": (896, I32), "KD": (48, BF),
+    "TK": (256, I32), "KIN": (192, I32), "WT": (4, I32), "TH": (4, I32), "WB": (8, BF),
+    "KM": (96, F32), "KN": (224, F32), "LK": (384, U16), "KA": (192, F32), "KB": (192, F32),
+    "MAT": (MW * len(MATS), BF), "IF": (128, F32), "CC": (48, F32), "CI": (8, I32), "IO": (MW, BF), "IOA": (128, BF),
+    "IOB": (128, BF), "KI": (128, BF), "VT": (400, F32), "DC": (48, BF), "M50": (400, BF), "C50": (400, F32),
+    "CZ": (256, H16), "N4": (128, BF), "AT": (144, BF),
     "DD": (256, H16), "CQ": (256, BF), "P0": (256, BF), "PF": (256, F32),
-    "TA": (2048, BF), "TB": (3072, BF), "TC": (3072, BF), "TR": (3072, BF), "TD": (2048, BF), "TE": (2048, BF),
+    "TA": (3072, BF), "TB": (3072, BF), "TC": (3072, BF), "TR": (3072, BF), "TD": (3072, BF), "TE": (3072, BF),
     "HM": (144, I32), "HC": (144, I32), "HD": (144, I32), "PO": (144, I32), "CL": (144, U16),
-    "DF": (2304, BF), "AB": (2304, BF), "NR": (144, F32), "SC": (144, F32), "M01": (48, F32),
-    "MX": (48, I32), "KEY": (48, I32), "KEYB": (48, BF), "CT": (56, I32), "IB": (392, BF), "S1": (392, BF),
-    "LE": (392, BF), "S2": (392, H16), "RM": (392, BF), "L1": (8, U16), "L2F": (8, F32), "L2": (8, U16),
-    "EE": (128, BF), "CV": (256, H16), "KE": (256, H16), "SL": (16, U16), "FL": (8, U16),
-    "Z0": (128, BF), "OX": (128, BF), "RG": (128, BF), "XN": (128, BF), "G": (128, I32), "U": (768, I32),
-    "VR": (128, F32), "TT": (128, F32), "N1": (128, F32), "N2": (128, H16),
-    "OV": (48, BF), "NG": (96, F32), "LS": (48, U16), "KP": (96, H16), "WR": (192, F32), "DEAD": (48, BF),
-    "WW": (2048, BF), "ONE": (512, BF), "HI": (128, BF), "NB": (136, BF), "RB": (768, BF),
+    "DF": (2304, BF), "AB": (2304, BF), "SG": (144, BF), "SC": (144, F32), "NR": (48, F32), "M01": (48, F32),
+    "MX": (48, I32), "CT": (56, I32), "KEY": (48, I32), "IB": (400, BF), "S1": (400, BF),
+    "S2": (400, F32), "RM": (400, BF), "L1": (8, U16), "L2F": (8, F32), "L2": (8, U16),
+    "EE": (128, BF), "CV": (256, H16), "KE": (256, H16), "SL": (16, U16), "NL": (48, U16),
+    "Z0": (128, BF), "OH": (128, BF), "RG": (128, BF),
+    "VR": (128, F32), "TT": (128, F32), "T2": (128, F32), "N1": (128, F32), "N2": (128, H16), "N3": (128, BF),
+    "DEAD": (48, BF), "WW": (3072, BF), "ONE": (400, BF), "HI": (128, BF), "NB": (128, BF), "DK": (2304, BF),
 }
 SCRATCH = {name: ("sbuf", [128, n], dtype) for name, (n, dtype) in SB.items()}
 for _b in range(8):
     SCRATCH["ps%d" % _b] = ("psum", [128, 512], F32)
 WIDTH = {BF: 2, H16: 2, U16: 2, F32: 4, I32: 4}
 NDMA = 24
-SEMAPHORES = ["sv", "ss", "sp", "sg", "rt_in", "tab_in", "hand_in", "sent"] + ["d%d" % i for i in range(NDMA)]
+SEMAPHORES = ["sv", "ss", "sp", "sg", "in_RT", "in_NTB", "in_QT", "hand_RT", "hand_NTB", "hand_QT", "sent"] + ["d%d" % i for i in range(NDMA)]
+SEMAPHORES += ["%s%d" % (nm, i) for nm in ("fold", "back") for i in range(12)]
 ESEM = {"v": "sv", "s": "ss", "p": "sp", "g": "sg"}
 
 COST = {"cyc": 1.04, "gat": 1.55, "sca": 3.8, "pe": 0.55, "vfix": 15.0, "sfix": 40.0, "hop": 120.0, "same": 60.0,
-        "rt_lat": 7000.0, "tab_lat": 11000.0, "dma": 1800.0, "rate": 250.0}
+        "RT": 7500.0, "NTB": 11000.0, "QT": 11000.0, "margin": 4000.0, "dma": 1800.0, "rate": 250.0,
+        "call": 1000.0, "fold": 4500.0, "foldcol": 1.0}
 PLAN = {
-    "first": [(128, "v"), (256, "v"), (384, "v"), (384, "v"), (256, "v"), (128, "v")],
-    "new": [[(192, "w"), (192, "w"), (192, "w"), (192, "w")], [(192, "w"), (192, "O"), (192, "w"), (192, "w")]],
-    "rest": [[(256, "v"), (256, "s"), (256, "v")], [(256, "m"), (256, "s"), (256, "w"), (256, "m"), (256, "w"), (256, "m")]],
-    "early": [[(256, "v")] * 3, [(256, "v")] * 6],
-    "late": [[(128, "v"), (256, "v"), (384, "v"), (256, "v"), (256, "v"), (256, "v")], [(384, "v")] * 4],
-    "last": [(384, "v"), (384, "o"), (384, "v"), (384, "v"), (384, "v"), (384, "o"), (384, "v"), (256, "v"), (128, "v")],
-    "dist": ["svsvvv", "vvsvvv"],
-    "patience": 300.0, "near": 0.5, "scalar": "ib",
+    "first": [(64, "o"), (128, "v"), (256, "v"), (512, "v"), (320, "v"), (256, "v")],
+    "new": [[(128, "O"), (256, "w"), (256, "w"), (128, "w")], [(192, "O"), (128, "m"), (192, "w"), (256, "w")]],
+    "rest": [[(256, "m"), (128, "m"), (128, "s"), (256, "s")],
+             [(64, "m"), (128, "s"), (128, "m"), (128, "m"), (192, "m")] + [(128, "m")] * 6 + [(128, "v")]],
+    "early": [[(256, "v"), (128, "v"), (384, "v")], [(448, "v"), (320, "v"), (384, "v"), (256, "v"), (128, "v")]],
+    "lnew": [[(256, "v"), (192, "v"), (320, "v")], [(384, "v")] * 2],
+    "lold": [[(256, "v")] * 3, [(384, "v")] * 2],
+    "last": [(256, "o"), (512, "v"), (512, "v"), (384, "v"), (384, "v"), (256, "v"), (384, "v"), (256, "v"), (128, "v")],
+    "banks": [3, 2, 3, 6],
+    "parts": [768],
+    "dist": [[[(384, "v"), (384, "v")], [(384, "s"), (384, "v")], [(384, "v"), (256, "v"), (128, "v")]],
+             [[(256, "v")] * 3, [(448, "s"), (320, "v")], [(448, "v"), (128, "v"), (192, "v")]]],
+    "nodes": [384, 384],
+    "patience": 1000.0, "near": 0.7, "wide": 3.0, "ahead": True, "scalar": "bpc", "turns": 3, "pace": 2.7, "sends": ["QT", "NTB"],
 }
 
 
@@ -91,11 +99,21 @@ def regs(r):
 
 
 def two_bytes(rs):
-    return all(WIDTH[SCRATCH[r[0]][2]] == 2 for r in rs)
+    return all(r[0] in SB and WIDTH[SB[r[0]][1]] == 2 for r in rs)
+
+
+def cut(u, w):
+    out = []
+    while u < w:
+        e = min(w, (u // E + 1) * E)
+        out.append((u, e))
+        u = e
+    return out
 
 
 def build(rank, C, plan):
     ops = []
+    row = [None]
 
     def add(eng, kind, args, out, ins, cost, **kw):
         rd, wr = [], []
@@ -108,6 +126,10 @@ def build(rank, C, plan):
                 wr.append(r)
         d = {"eng": eng, "kind": kind, "args": args, "rd": rd, "wr": wr, "cost": cost, "lat": 0.0, "at": 0.0}
         d.update(kw)
+        if row[0] and any(isinstance(r, tuple) and r[0] == "@" and r[2][0] in ("LK", "CL") for r in ins):
+            d["row"] = row[0]
+        if out and out[0][0] == "AB":
+            d["row"] = row[0] + "abs"
         ops.append(d)
 
     def vcost(out, in0, full):
@@ -142,13 +164,18 @@ def build(rank, C, plan):
         add("s", "act", (out, in0, func, bias, scale), [out], [in0, bias, scale], c)
 
     def mm(out, pairs, start=True, stop=True):
-        ins = []
+        ins = [] if start else [out]
+        c = 30.0
         for l, r in pairs:
             ins += [l, r]
-        add("p", "mm", (out, pairs, start, stop), [out], ins, 30.0 + len(pairs) * max(64, ncols(out)) * C["pe"])
+            c += max(64, ncols(out)) * C["pe"] * (1 if two_bytes([l]) else 4)
+        add("p", "mm", (out, pairs, start, stop), [out], ins, c)
 
     def iota(out, pattern, base, mult=0):
         add("g", "iota", (out, pattern, base, mult), [out], [], 130.0 + 2 * ncols(out) * C["cyc"])
+
+    def keep(out, in0, pattern, base, mult=0):
+        add("g", "sel", (out, in0, pattern, AL.is_ge, 0.0, base, mult), [out], [in0], 170.0 + 2 * ncols(out) * C["cyc"])
 
     def fill(out, val):
         iota(out, [[0, ncols(out)]], val)
@@ -165,157 +192,181 @@ def build(rank, C, plan):
         else:
             ts(M(name, 0, n), src, col, AL.is_equal, scale, AL.mult)
 
-    nd = [0, 0]
+    nd = [0, 0, 0, 0]
+
+    def bank(kind="L"):
+        nd[2] += 1
+        return "ps%s%d" % (kind, nd[2])
 
     def dma(q, kind, sb, dr, nbytes):
-        nd[1] = nd[1] + nbytes if kind == "load" else nbytes
-        add(q, kind, (sb, dr), [sb] if kind == "load" else [], [] if kind == "load" else [sb], 60.0,
-            lat=C["dma"] + nd[1] / C["rate"], sem="d%d" % nd[0])
+        if kind == "load":
+            nd[1] += nbytes
+            add(q, kind, (sb, dr), [sb], [], 60.0, lat=C["dma"] + nd[1] / C["rate"], sem="d%d" % nd[0])
+        else:
+            add(q, kind, (sb, dr), [], [sb], 60.0 + nbytes / C["rate"], lat=C["dma"], sem="d%d" % nd[0])
         nd[0] += 1
 
     own = rank * NT
     cc = lambda j: R("CC", j, j + 1)
+    dma("s", "load", R("RT", own, own + NT), ("rx",), 65536)
     dma("s", "load", R("KIN", 0, 96), ("k0",), 49152)
     dma("s", "load", R("KIN", 96, 192), ("k1",), 49152)
-    dma("s", "load", R("RT", own, own + NT), ("rx",), 65536)
     dma("y", "load", R("X", O, O + V0), ("x0",), 393216)
+    dma("s", "load", R("WT", 0, 1), ("wt",), 8192)
+    dma("s", "load", R("TH", 0, 1), ("th",), 8192)
     dma("y", "load", W("TK"), ("tk",), 131072)
     dma("y", "load", W("NX"), ("nx",), 393216)
-    dma("y", "load", R("WT", 0, 1), ("wt",), 8192)
-    dma("y", "load", R("TH", 0, 1), ("th",), 8192)
     iota(R("CI", 0, 1), [[0, 1]], 0, 1)
-    iota(W("IO"), [[1, 146]], 0)
+    iota(W("IO"), [[1, MW]], 0)
     iota(W("IOA"), [[16, 8], [0, 16]], 0)
     iota(W("IOB"), [[16, 8], [0, 8], [128, 2]], 0)
-    add("g", "send", ("RT",), [], [R("RT", own, own + NT)], 1500.0, lat=C["rt_lat"])
+    add("g", "send", ("RT",), [], [R("RT", own, own + NT)], 1500.0, lat=C["RT"])
     for o in range(8):
         if o != rank:
-            add("x", "arrive", ("rt_in",), [R("RT", o * NT, o * NT + NT)], [], 0.0, sem="rt_in")
-            add("x", "arrive", ("tab_in",), [R("NTB", o * NT, o * NT + NT), R("QT", o * NT, o * NT + NT)], [], 0.0, sem="tab_in")
-    ms(R("X", 0, O), 0.0); ms(R("P", 0, O), 0.0)
+            for nm in ("RT", "NTB", "QT"):
+                add("x", "arrive", (nm,), [R(nm, o * NT, o * NT + NT)], [], 0.0, sem="in_" + nm)
+    ms(R("X", 0, O), 0.0); ms(R("P", 0, O), 0.0); ms(W("KN"), -4096.0)
     ts(W("KA"), W("KIN"), -1024.0, AL.add)
     ts(W("KB"), W("KIN"), -8.0, AL.mult, 20480.0, AL.add)
-    for j in range(2):
-        for b in range(2):
+    for b in range(2):
+        for j, out in enumerate((R("KM", 48 * b, 48 * b + 48), R("KN", 56 * b, 56 * b + 48))):
             k = 96 * b + 48 * j
-            tt(KL("KM", b, E * j, E * j + E), R("KA", k, k + 48), R("KB", k, k + 48), AL.min)
-        ts(R("LK", 96 * j, 96 * j + 96), R("KM", 96 * j, 96 * j + 96), 1024.25 + O, AL.add)
+            tt(out, R("KA", k, k + 48), R("KB", k, k + 48), AL.min)
+        ts(R("LK", 96 + 48 * b, 144 + 48 * b), R("KN", 56 * b, 56 * b + 48), 1024.25 + O, AL.add)
+    ts(R("LK", 0, 96), W("KM"), 1024.25 + O, AL.add)
     ts(R("CI", 1, 2), R("CI", 0, 1), 15, AL.bitwise_and)
     ts(R("CI", 2, 3), R("CI", 0, 1), 1, AL.logical_shift_right, 7, AL.bitwise_and)
     ts(R("CI", 3, 4), R("CI", 0, 1), 1, AL.bitwise_and)
     cp(R("CC", 0, 4), R("CI", 0, 4))
     io = R("IO", 0, 128)
     ts(M("I"), io, cc(0), AL.is_equal)
-    for nm, sc in (("nI", -1.0), ("Ih", HALF), ("IW0", UP - 1.0), ("IW1", 2.0), ("I16", 16.0), ("I256", 256.0), ("I4k", 4096.0),
-                   ("I64k", 65536.0), ("I1m", 1048576.0), ("Iq", 1.0 / 2048.0), ("nIq", -1.0 / 2048.0), ("nI4k", -4096.0)):
+    for nm, sc in (("nI", -1.0), ("Ih", HALF), ("IW0", UP - 1.0), ("IW1", UP - 2 * UP * HALF - 1.0), ("I256", 256.0),
+                   ("I16", 16.0), ("I4k", 4096.0), ("I64k", 65536.0), ("I1m", 1048576.0), ("Iq", 1.0 / 2048.0), ("nIq", -1.0 / 2048.0), ("IB", 5120.0)):
         mat("i", nm, 128, io, cc(0), "I", sc)
+    act(W("IF"), M("I"), AF.Copy)
     tt(cc(4), cc(0), cc(1), AL.subtract)
     aff(cc(5), cc(4), 1.0, 15.0)
     aff(cc(7), cc(2), 1.0, -16.0)
     ts(cc(8), cc(1), 14.0, AL.is_equal)
     io3 = R("IO", 0, 143)
     ts(M("B1", 0, 143), io3, cc(5), AL.is_equal)
-    mat("b", "B14", 143, io3, cc(5), "B1", cc(8))
     ts(M("BO"), W("IOA"), cc(4), AL.is_equal)
     mat("b", "BO14", 128, W("IOA"), cc(4), "BO", cc(8))
-    mat("b", "BOn", 128, W("IOA"), cc(4), "BO", -16384.0)
-    mat("b", "BO6", 128, W("IOA"), cc(4), "BO", 6.0)
+    ms(W("ONE"), 1.0)
+    for nm, sc in (("nBO", -1.0), ("nBO6", -6.0), ("nBOk", -1024.0)):
+        mat("b", nm, 128, W("IOA"), cc(4), "BO", sc)
     ts(W("CQ"), W("TK"), 6.0, AL.min, -16.0, AL.add)
     ts(W("DD"), W("TK"), -6.0, AL.add, 0.0, AL.max)
-    ts(W("P0"), W("TK"), 0.0, AL.is_equal, -8192.0, AL.mult)
-    mm(R("ps6", 0, NT), [(M("BO14"), W("CQ"))])
-    mm(R("ps7", 0, NT), [(M("Iq"), W("CQ")), (M("nI"), W("DD")), (M("I"), W("P0"))])
-    ts(W("PF"), R("ps6", 0, NT), cc(7), AL.is_equal, -16384.0, AL.mult)
-    tt(R("QT", own, own + NT), R("ps7", 0, NT), W("PF"), AL.min)
-    mm(R("ps5", 0, NT), [(M(n), R("NX", w * NT, w * NT + NT)) for w, n in enumerate(("I", "I16", "I256", "I4k", "I64k", "I1m"))])
-    act(R("NTB", own, own + NT), R("ps5", 0, NT), AF.Copy)
-    add("g", "send", ("NTB",), [], [R("NTB", own, own + NT)], 1000.0, lat=C["tab_lat"])
-    add("g", "send", ("QT",), [], [R("QT", own, own + NT)], 1000.0, lat=C["tab_lat"])
-    cp(cc(9), R("WT", 0, 1)); cp(cc(10), R("TH", 0, 1)); cp(R("WB", 0, 1), R("WT", 0, 1))
+    if "p" in plan["scalar"]:
+        act(W("P0"), W("CQ"), AF.Relu, -15.0 * 8192.0, -8192.0)
+    else:
+        ts(W("P0"), W("CQ"), -16.0, AL.is_equal, 8192.0, AL.mult)
+    p1, p2 = R(bank(), 0, NT), R(bank(), 0, NT)
+    mm(p1, [(M("BO14"), W("CQ"))])
+    mm(p2, [(M("Iq"), W("CQ")), (M("nI"), W("DD")), (M("nI"), W("P0"))])
+    ts(W("PF"), p1, cc(7), AL.is_equal, -16384.0, AL.mult)
+    tt(R("QT", own, own + NT), p2, W("PF"), AL.min)
+    p1 = R(bank(), 0, NT)
+    mm(p1, [(M(n), R("NX", w * NT, w * NT + NT)) for w, n in enumerate(("I", "I16", "I256", "I4k", "I64k", "I1m"))])
+    act(R("NTB", own, own + NT), p1, AF.Copy)
+    for nm in plan["sends"]:
+        add("g", "send", (nm,), [], [R(nm, own, own + NT)], 1000.0, lat=C[nm])
+    cp(cc(9), R("WT", 0, 1)); ts(cc(10), R("TH", 0, 1), -0.5, AL.add); cp(R("WB", 0, 1), R("WT", 0, 1))
     mat("b", "BW", 143, io3, cc(5), "B1", cc(9))
-    mm(R("ps6", 0, 1), [(M("BO"), R("WB", 0, 1))])
-    act(cc(24), R("ps6", 0, 1), AF.Copy, 0.0, -UP)
-    ts(W("UT"), io, cc(0), AL.is_lt, -1.0, AL.mult)
-    ts(W("UU"), io, cc(0), AL.is_equal, 1024.0, AL.mult)
-    tt(W("UT"), W("UT"), W("UU"), AL.add)
-    tt(M("UN"), W("UT"), M("BO"), AL.mult)
+    p1 = R(bank(), 0, 1)
+    mm(p1, [(M("BO"), R("WB", 0, 1))])
+    act(cc(24), p1, AF.Copy, 0.0, -UP)
+    keep(M("nU"), M("nBO"), [[-1, 128]], -1, 1)
+    fill(W("N4"), -4)
     fill(R("RT", 2048, 2064), 0)
-    fill(W("M49"), 1); fill(R("M49", 0, 392, 49), 0); fill(R("IB", 48, 392, 49), 1)
+    keep(W("M50"), R("ONE", 0, 400), [[0, 8], [1, 50]], -1); fill(R("IB", 0, 400, 50), 0); fill(R("IB", 49, 400, 50), 1)
+    u = 0
+    for n in plan["parts"]:
+        iota(R("AT", 3 * u // 16, 3 * (u + n) // 16), [[-4096, 3], [0, n // 16]], 5120)
+        u += n
     iota(W("KI"), [[0, 8], [1, 16]], 1)
-    iota(W("VT"), [[0, 8], [16, 49]], 0)
-    fill(R("CT", 48, 56), 2048); fill(R("NTB", 2048, 2056), 0); fill(R("KM", 192, 384), 0)
+    iota(W("VT"), [[0, 8], [16, 50]], -16)
+    fill(R("CT", 48, 56), 2048); fill(R("QT", 2048, 2056), -16384); fill(R("NTB", 2048, 2056), 0)
     for j in range(4):
         fill(R("X", O + V0 + 384 * j, O + V0 + 384 * j + 384), int(UP))
+    for j in range(6):
+        fill(R("DK", 384 * j, 384 * j + 384), 0)
     iota(W("DC"), [[0, 8], [16, 6]], 0)
-    act(R("QT", 2048, 2056), R("IO", 0, 8), AF.Identity, cc(8), 0.0)
-    act(R("QT", 2048, 2056), R("QT", 2048, 2056), AF.Identity, -8192.0, 8192.0 - 14.0 / 2048.0)
     aff(cc(6), cc(4), 1.0, 128.0)
-    aff(cc(11), cc(1), 6.0, 0.0)
     aff(cc(12), cc(1), -6.0, 858.0)
-    aff(cc(25), cc(1), 1.0, 0.5)
-    ts(M("L0"), W("IOB"), cc(4), AL.is_equal)
-    ts(M("L1"), W("IOB"), cc(6), AL.is_equal)
+    aff(cc(25), cc(1), 1024.0, 512.0)
+    aff(cc(11), cc(2), 128.0, 0.0)
+    for b, col in ((0, 4), (1, 6)):
+        ts(M("L%d" % b), W("IOB"), cc(col), AL.is_equal)
     act(W("VT"), W("VT"), AF.Identity, cc(1), 1.0)
-    act(R("VT", 48, 392, 49), R("IO", 0, 8), AF.Identity, cc(12), 96.0)
+    act(R("VT", 49, 400, 50), R("IO", 0, 8), AF.Identity, cc(12), 96.0)
     act(W("DC"), W("DC"), AF.Identity, cc(1), 1.0)
-    ts(W("D49"), W("M49"), 0.0, AL.mult)
-    ts(R("D49", 0, 392, 49), R("IO", 0, 8), 98.0, AL.mult, 48.0, AL.add)
+    act(W("KD"), R("VT", 1, 49), AF.Identity, 128.0 - 5.0 / 12.0, 1.0 / 6.0)
+    iota(W("C50"), [[1, 400]], 0)
+    ts(M("DI"), io, cc(0), AL.is_equal, cc(25), AL.mult)
     for t in range(RO):
         ts(R("CZ", 128 * t, 128 * t + 128), io, 6.0, AL.mult, float(V0 + E * t - 1024), AL.add)
-    ts(W("CF"), R("IO", 0, 8), 96.0, AL.mult, cc(11), AL.add)
     ts(cc(13), cc(2), 1.0, AL.max, 6.0, AL.min)
     aff(cc(14), cc(2), 501.0, cc(5))
     aff(cc(15), cc(13), -500.0, cc(14))
-    aff(cc(16), cc(3), 1000.0, -2.0)
-    aff(cc(17), cc(3), -1000.0, 998.0)
+    aff(cc(16), cc(3), 1000.0, 0.0)
+    aff(cc(17), cc(3), -1000.0, 1000.0)
     aff(cc(26), cc(16), 1.0, cc(15))
     aff(cc(27), cc(17), 1.0, cc(15))
-    for j, (val, op) in enumerate(((9.5, AL.is_lt), (9.5, AL.is_gt), (5.5, AL.is_lt), (5.5, AL.is_gt))):
-        ts(cc(18 + j), cc(1), val, op)
-    ts(cc(28), cc(1), 3.5, AL.is_lt)
-    ts(cc(23), cc(28), cc(3), AL.mult)
-    aff(cc(22), cc(23), -1.0, cc(28))
-    fill(W("ONE"), 1)
-    fill(R("NB", 0, 8), 0)
-    ts(cc(29), cc(1), 1.5, AL.is_lt)
-    ts(cc(30), cc(29), 2.0, AL.mult, cc(28), AL.subtract)
+    ts(R("CC", 32, 34), R("IO", 2, 5, 2), cc(1), AL.is_gt, -1.0, AL.mult)
+    ts(cc(23), cc(33), cc(3), AL.mult)
+    aff(cc(22), cc(23), -1.0, cc(33))
     aff(cc(31), cc(0), 1.0, 2.0)
-    mat("i", "D01", 128, io, cc(0), "I", cc(29))
-    mat("i", "A2", 128, io, cc(0), "I", cc(30))
-    ts(M("A1"), io, cc(31), AL.is_equal, cc(29), AL.mult)
+    ts(M("A3"), io, cc(31), AL.is_equal, cc(32), AL.mult)
+    ts(M("nD"), io, cc(0), AL.is_equal, cc(32), AL.mult)
     for b in range(2):
-        ts(M("K%d" % b, 0, 146), W("IO"), cc(26 + b), AL.is_equal)
-        for j, x in enumerate("abcd"):
-            mat("k", "K%d%s" % (b, x), 146, W("IO"), cc(26 + b), "K%d" % b, cc(18 + j))
+        ts(M("K%d" % b, 0, MW), W("IO"), cc(26 + b), AL.is_equal)
+        for x, step, base in (("a", -1, 3), ("b", 1, -4), ("c", -1, 1), ("d", 1, -2)):
+            keep(M("K%d%s" % (b, x), 0, MW), M("K%d" % b, 0, MW), [[0, MW // 16], [step, 16]], base)
         mat("b", "B%dr" % b, 143, io3, cc(5), "B1", cc(22 + b))
 
-    rot = {}
+    def sums(n, kind="A"):
+        return R(bank(kind), 0, n)
 
-    def nxt(k, n):
-        rot[k] = (rot.get(k, 0) + 1) % n
-        return rot[k]
+    def diffs(n):
+        return R(bank("D"), 0, n)
 
-    def bank():
-        return "ps%d" % (5 + nxt("m", 3))
+    def pair(table, S, u, w, first, out, alone):
+        for a, b in cut(u, w):
+            f = R(first[0], first[1] + a - u, first[1] + b - u)
+            g0, g1 = (IND(R(table, 0, O + S), KL("LK", k, a, b)) for k in range(2))
+            if alone:
+                cp(f, g0)
+            else:
+                act(f, g0, AF.Copy)
+            tt(R(out[0], out[1] + a - u, out[1] + b - u), g1, f, AL.max)
 
-    def tmp(name, n):
-        k = 512 * nxt(name, SB[name][0] // 512)
-        return R(name, k, k + n)
+    def folded(table, S, u, w, names, less, more, out, both):
+        for a, b in cut(u, w):
+            for k, nm in enumerate(names):
+                gk = IND(R(table, 0, O + S), KL("LK", k, a, b))
+                if k == 0 or both:
+                    act(R(nm, a, b), gk, AF.Identity, -less, 1.0)
+                else:
+                    ts(R(nm, a, b), gk, -less, AL.add)
+        srcs = [R(nm, u, w) for nm in names] + more
+        add("g", "fold", (out, srcs, nd[3]), [out], srcs, C["call"], lat=C["fold"] + (w - u) * C["foldcol"] * (len(srcs) + 1),
+            sem="back%d" % nd[3])
+        nd[3] += 1
 
     def stage1(u, S, pieces):
         for n, how in pieces:
             w = u + n
-            ta, pp = tmp("TA", n), R("P", O + u, O + w)
-            g0, g1 = (IND(R("X", 0, O + S), KL("LK", b, u, w)) for b in range(2))
-            if how == "o":
-                cp(ta, g0)
+            ta, pp = R("TA", u, w), R("P", O + u, O + w)
+            if how == "f":
+                folded("X", S, u, w, ("TA", "TD"), 0.0, [], pp, True)
+            elif how != "s":
+                pair("X", S, u, w, ta, pp, how == "o")
             else:
+                g0, g1 = (IND(R("X", 0, O + S), KL("LK", b, u, w)) for b in range(2))
+                td, te = R("TD", u, w), R("TE", u, w)
+                pd, pa = diffs(n), sums(n)
                 act(ta, g0, AF.Copy)
-            if how != "s":
-                tt(pp, g1, ta, AL.max)
-            else:
-                td, te = tmp("TD", n), tmp("TE", n)
-                pd = R("ps%d" % (3 + nxt("d", 2)), 0, n); pa = R("ps%d" % nxt("a", 3), 0, n)
                 act(td, g1, AF.Copy)
                 mm(pd, [(M("nI"), ta), (M("I"), td)])
                 act(te, pd, AF.Relu)
@@ -326,105 +377,143 @@ def build(rank, C, plan):
     def stage2(u, S, pieces, sweep):
         for n, how in pieces:
             w = u + n
-            tb, tc, tr = tmp("TB", n), tmp("TC", n), tmp("TR", n)
-            if sweep == RO:
-                pa = R("ps%d" % (0, 1, 2, 5, 6)[nxt("a5", 5)], 0, n); pd = R("ps%d" % (3, 4, 7)[nxt("d3", 3)], 0, n)
-            else:
-                pa = R("ps%d" % nxt("a", 3), 0, n); pd = R("ps%d" % (3 + nxt("d", 2)), 0, n)
+            tb, tc, tr = (R(nm, u, w) for nm in ("TB", "TC", "TR"))
+            pd, pa = diffs(n), sums(n)
             xs, pp = R("X", O + u, O + w), R("P", O + u, O + w)
-            g0, g1 = (IND(R("P", 0, O + S), KL("LK", b, u, w)) for b in range(2))
             lift = UP if sweep == 0 else UP - 2 * UP * HALF
-            if how in "oO":
-                cp(tb, g0)
-            else:
-                act(tb, g0, AF.Copy)
+            if how in "fg":
+                folded("P", S, u, w, ("TB", "TC"), 2.0, [pp], tr, how == "f")
+                for a in range(u, w, 512):
+                    b = min(w, a + 512)
+                    pa = sums(b - a)
+                    mm(pa, [(M("Ih"), R("X", O + a, O + b)), (M("Ih"), R("TR", a, b))])
+                    act(R("X", O + a, O + b), pa, AF.Identity, lift, 1.0)
+                u = w
+                continue
             if how in "wO":
-                ww = tmp("WW", n)
+                ww = R("WW", u, w)
                 mm(pd, [(M("Ih"), xs), (M("Ih"), pp)])
                 act(ww, pd, AF.Identity, lift, 1.0)
                 mm(pa, [(M("IW%d" % sweep), R("ONE", 0, n)), (M("Ih"), xs)], True, False)
-                tt(tc, g1, tb, AL.max)
+                pair("P", S, u, w, tb, tc, how == "O")
                 mm(pa, [(M("Ih"), tc)], False, True)
                 tt(xs, pa, ww, AL.max)
                 u = w
                 continue
             mm(pa, [(M("Ih"), xs), (M("Ih"), pp)], True, False)
             if how == "s":
-                te = tmp("TE", n)
+                g0, g1 = (IND(R("P", 0, O + S), KL("LK", b, u, w)) for b in range(2))
+                te = R("TE", u, w)
+                act(tb, g0, AF.Copy)
                 act(tc, g1, AF.Copy)
                 mm(pd, [(M("nI"), tb), (M("I"), tc)])
                 act(te, pd, AF.Relu)
                 mm(pd, [(M("nI"), pp), (M("I"), tb), (M("I"), te)])
             else:
-                tt(tc, g1, tb, AL.max)
+                pair("P", S, u, w, tb, tc, how == "o")
                 mm(pd, [(M("nI"), pp), (M("I"), tc)])
             act(tr, pd, AF.Relu, -2.0, 1.0)
             mm(pa, [(M("Ih"), tr)], False, True)
-            if sweep == RO:
-                ts(xs, pa, CR, AL.add, -CR - 2 * UP * HALF, AL.add)
-                dma("y", "store", xs, ("y", u, w), 256 * n)
-            elif how in "vo":
+            if how in "vo":
                 ts(xs, pa, lift, AL.add)
             else:
                 act(xs, pa, AF.Identity, lift, 1.0)
             u = w
 
+    def last(pieces):
+        w = 0
+        for j, (n, how) in enumerate(pieces):
+            u, w = w, w + n
+            tb, tc, tr = (R(nm, u, w) for nm in ("TB", "TC", "TR"))
+            pa, pd = sums(n, "Z"), diffs(n)
+            xs, pp = R("X", O + u, O + w), R("P", O + u, O + w)
+            if how in "fg":
+                folded("P", A, u, w, ("TB", "TC"), 2.0, [pp], tr, how == "f")
+                mm(pa, [(M("Ih"), xs), (M("Ih"), tr)])
+            else:
+                mm(pa, [(M("Ih"), xs), (M("Ih"), pp)], True, False)
+                mm(pd, [(M("nI"), pp)], True, False)
+                pair("P", A, u, w, tb, tc, how == "o")
+                mm(pd, [(M("I"), tc)], False, True)
+                act(tr, pd, AF.Relu, -2.0, 1.0)
+                mm(pa, [(M("Ih"), tr)], False, True)
+            ts(xs, pa, CR, AL.add, -CR - 2 * UP * HALF, AL.add)
+            dma("y", "store", xs, ("y", u, w), 256 * n)
+            ops[-1]["at"] = (A - w) * plan["pace"]
+
     def sel(base, src, a, n):
         return [(M(base, 15 - r), R(src, a + r, a + n, 16)) for r in range(16)]
 
+    row[0] = "first"
     stage1(0, V0, plan["first"])
     fill(R("X", 0, O), int(UP))
     for t in range(RO):
         S = V0 + E * t
         nw = O + S - E
         kc = 96 * (t + 1)
+        row[0] = "new%d" % t
         stage2(S - E, S, plan["new"][t], t)
-        pb = bank()
-        mm(R(pb, 0, 48), sel("BW", "X", nw, E))
-        for m in range(3):
-            ts(R("HM", 48 * m, 48 * m + 48), R(pb, 0, 48), cc(24), AL.add, float(97 * m + 31 * t), AL.add)
-        ts(W("HC"), W("HM"), 2047, AL.bitwise_and)
-        ts(W("HD"), W("HC"), 2049.0, AL.mult)
-        ts(W("PO"), W("HD"), 3, AL.logical_shift_right, 2047, AL.bitwise_and)
-        cp(W("CL"), W("PO"))
-        for m in range(3):
-            for h in range(2):
-                a = E * m + 384 * h
-                gr = IND(W("RT"), R("CL", 48 * m + 24 * h, 48 * m + 24 * h + 24))
-                xs, df, ab = R("X", nw + 384 * h, nw + 384 * h + 384), R("DF", a, a + 384), R("AB", a, a + 384)
-                if plan["dist"][t][2 * m + h] == "v":
-                    tt(df, gr, xs, AL.subtract)
-                    act(ab, df, AF.Abs, UP, 1.0)
-                else:
-                    pd = R("ps%d" % (3 + nxt("d", 2)), 0, 384)
-                    act(df, gr, AF.Copy)
-                    mm(pd, [(M("nI"), xs), (M("I"), df)])
-                    act(ab, pd, AF.Abs, UP, 1.0)
+        u = 0
+        row[0] = "far%d" % t
+        for h, n in enumerate(plan["parts"]):
+            c, k = u // 16, n // 16
+            at = lambda nm, a, b: R(nm, 3 * c + a * k, 3 * c + b * k)
             pb = bank()
-            mm(R(pb, 0, 48), ([(M("I256"), W("DEAD"))] if t else []) + sel("B1", "AB", E * m, E))
-            nr, sc = R("NR", 48 * m, 48 * m + 48), R("SC", 48 * m, 48 * m + 48)
-            ts(nr, R(pb, 0, 48), cc(10), AL.is_lt, 2048.0 * (5 - 2 * m), AL.mult)
-            tt(sc, nr, R("PO", 48 * m, 48 * m + 48), AL.add)
-            if m == 1:
-                tt(W("M01"), R("SC", 0, 48), R("SC", 48, 96), AL.max)
-        tt(W("MX"), W("M01"), R("SC", 96, 144), AL.max)
+            mm(R(pb, 0, k), sel("BW", "X", nw + u, n))
+            for m in range(3):
+                ts(at("HM", m, m + 1), R(pb, 0, k), cc(24), AL.add, float(97 * m + 31 * t), AL.add)
+            for a, b in ((0, 1), (1, 3)) if plan["ahead"] else ((0, 3),):
+                ts(at("HC", a, b), at("HM", a, b), 2047, AL.bitwise_and)
+                ts(at("HD", a, b), at("HC", a, b), 2049.0, AL.mult)
+                ts(at("PO", a, b), at("HD", a, b), 3, AL.logical_shift_right, 2047, AL.bitwise_and)
+                cp(at("CL", a, b), at("PO", a, b))
+            pb, pl = bank(), bank()
+            end = u + n == E
+            for m in range(3):
+                a = 0
+                for w, how in plan["dist"][t][3 * h + m]:
+                    gr = IND(W("RT"), R("CL", 3 * c + m * k + a // 16, 3 * c + m * k + (a + w) // 16))
+                    d = E * m + u + a
+                    xs, df, ab = R("X", nw + u + a, nw + u + a + w), R("DF", d, d + w), R("AB", d, d + w)
+                    if how == "v":
+                        tt(df, gr, xs, AL.subtract)
+                        act(ab, df, AF.Abs, UP, 1.0)
+                    else:
+                        pd = diffs(w)
+                        act(df, gr, AF.Copy)
+                        mm(pd, [(M("nI"), xs), (M("I"), df)])
+                        act(ab, pd, AF.Abs, UP, 1.0)
+                    a += w
+                mm(R(pl, 0, k) if end and m == 2 else R(pb, m * k, m * k + k),
+                   ([(M("I256"), R("DEAD", c, c + k))] if t else []) + sel("B1", "AB", E * m + u, n))
+                if m == 2 - end:
+                    j = m + 1
+                    act(at("SG", 0, j), R(pb, 0, j * k), AF.Sign, cc(10), -1.0)
+                    mm(R(pb, 0, j * k), [(M("I"), at("AT", 0, j)), (M("IB"), at("SG", 0, j))])
+                    tt(at("SC", 0, j), R(pb, 0, j * k), at("PO", 0, j), AL.add)
+                    tt(R("M01", c, c + k), at("SC", 0, 1), at("SC", 1, 2), AL.max)
+            if end:
+                ts(R("NR", 0, k), R(pl, 0, k), cc(10), AL.is_lt, 2048.0, AL.mult)
+                tt(at("SC", 2, 3), R("NR", 0, k), at("PO", 2, 3), AL.add)
+            tt(R("MX", c, c + k), R("M01", c, c + k), at("SC", 2, 3), AL.max)
+            u += n
         ts(W("KEY"), W("MX"), 8, AL.logical_shift_right, 15, AL.bitwise_and)
         for o in range(8):
-            ts(R("IB", 49 * o, 49 * o + 48), W("KEY"), float(8 + o), AL.is_equal)
-        scan(W("S1"), W("M49"), W("IB"), AL.mult, AL.add)
+            ts(R("IB", 50 * o + 1, 50 * o + 49), W("KEY"), float(8 + o), AL.is_equal)
+        scan(W("S1"), W("M50"), W("IB"), AL.mult, AL.add)
         ts(R("CT", 0, 48), W("MX"), 2047, AL.bitwise_and)
-        cp(W("KEYB"), W("KEY"))
-        p1, p2 = bank(), bank()
-        mm(R(p1, 0, 392), [(M("BO"), W("S1"))])
-        mm(R(p2, 0, 392), [(M("UN"), W("IB")), (M("BO"), W("S1"))])
-        act(W("LE"), R(p1, 0, 392), AF.Sign, cc(25), -1.0)
-        act(W("RM"), R(p2, 0, 392), AF.Relu, -1024.0, 1.0)
-        scan(W("S2"), W("D49"), W("LE"), AL.max, AL.add)
-        s2 = R("S2", 47, 392, 49)
-        ts(W("L1"), s2, 0.5, AL.mult, 0.25, AL.add)
+        p1, p2 = R(bank(), 0, 400), R(bank(), 0, 400)
+        mm(p1, [(M("DI"), R("ONE", 0, 400))], True, False)
+        mm(p2, [(M("nU"), W("IB")), (M("I4k"), W("IB"))], True, False)
+        mm(p1, [(M("nBOk"), W("S1"))], False, True)
+        mm(p2, [(M("BO"), W("S1"))], False, True)
+        act(W("RM"), p2, AF.Relu, -4096.0, 1.0)
+        scan(W("S2"), W("C50"), p1, AL.min, AL.max)
+        s2 = R("S2", 49, 400, 50)
+        ts(W("L1"), s2, 0.25, AL.add)
         tt(W("EE"), IND(W("RM"), W("L1")), W("KI"), AL.is_equal)
-        tt(W("L2F"), s2, R("D49", 0, 392, 49), AL.subtract)
-        ts(W("L2"), W("L2F"), 0.5, AL.mult, 24.25, AL.add)
+        tt(W("L2F"), s2, R("C50", 0, 400, 50), AL.subtract)
+        ts(W("L2"), W("L2F"), -0.75, AL.add)
         tt(R("CV", 128, 256), IND(W("VT"), W("L1")), W("EE"), AL.mult)
         tt(R("CV", 0, 128), IND(W("CT"), W("L2")), W("EE"), AL.mult)
         pb = bank()
@@ -432,77 +521,95 @@ def build(rank, C, plan):
         ts(W("SL"), R(pb, 0, 16), 0.25, AL.add)
         cl, vl = R("SL", 0, 8), R("SL", 8, 16)
         pv = bank()
-        mm(R(pv, 0, 128), [(M("BO"), R("CV", 128, 256))])
-        act(W("VR"), R(pv, 0, 128), AF.Identity, float(S - E - 1024), 1.0)
+        if "t" not in plan["scalar"]:
+            mm(R(pv, 0, 128), [(M("BO"), R("CV", 128, 256))])
+            act(W("VR"), R(pv, 0, 128), AF.Identity, float(S - E - 1024), 1.0)
         for b in range(2):
-            tt(R("KE", 128 * b, 128 * b + 128), IND(R("KM", kc + 48 * b, kc + 48 * b + 56), W("L2")), W("EE"), AL.mult)
-        pr = bank()
-        rm = [(M("I"), R("RM", 49 * o, 49 * o + 48)) for o in range(8)]
-        mm(R(pr, 0, 48), rm)
-        act(W("OV"), R(pr, 0, 48), AF.Relu, -16.0, 1.0)
-        for b in range(2):
-            mm(R(pr, 48 * b, 48 * b + 48), [(M("I16"), W("KEYB"))] + rm + [(M("nI4k"), W("OV"))])
-        ts(W("LS"), R(pr, 0, 48), -129.0 + 8.25, AL.add)
-        ts(W("NG"), R(pr, 0, 96), 128.5, AL.is_lt)
-        tt(W("KP"), R("KM", kc, kc + 96), W("NG"), AL.mult)
+            tt(R("KE", 128 * b, 128 * b + 128), IND(R("KN", 112 * t + 56 * b, 112 * t + 56 * b + 56), W("L2")), W("EE"), AL.mult)
+        xw = R("X", nw, nw + 2 * E)
+        act(W("OH"), IND(xw, vl), AF.Identity, 110.0 - UP / 2, 0.5)
+        if "r" in plan["scalar"]:
+            act(W("RG"), IND(W("RT"), cl), AF.Identity, UP - 110.25, 0.5)
+        else:
+            ts(W("RG"), IND(W("RT"), cl), 0.5, AL.mult, UP - 110.25, AL.add)
+        tt(IND(xw, vl), W("OH"), W("RG"), AL.add)
+        ts(R("U", 0, 128), W("OH"), 2.0, AL.mult, -220.0, AL.add)
         if t + 1 < RO:
             pb = bank()
+            mm(R(pb, 0, 48), [(M("I"), W("DC"))], True, False)
             for c6 in range(6):
-                mm(R(pb, c6, 48, 6), [(M("BO6"), R("S1", 47, 392, 49))])
-            tt(W("DEAD"), R(pb, 0, 48), W("DC"), AL.is_le)
+                mm(R(pb, c6, 48, 6), [(M("nBO6"), R("S1", 48, 400, 50))], False, c6 == 5)
+            act(W("DEAD"), R(pb, 0, 48), AF.Relu, 1.0, 1.0)
         act(W("Z0"), IND(W("QT"), cl), AF.Identity, 15.0, 2048.0)
-        tt(W("TT"), IND(W("QT"), cl), W("VR"), AL.add)
         pz, pu = bank(), bank()
+        old = [R("KE", 0, 128), R("KE", 128, 256)]
         mm(R(pz, 0, 128), [(M("I"), R("CZ", 128 * t, 128 * t + 128)), (M("I"), W("Z0"))])
-        mm(R(pu, 0, 128), [(M("BOn"), W("EE")), (M("L0"), R("KE", 0, 128)), (M("L1"), R("KE", 128, 256)), (M("nIq"), W("Z0"))])
-        tt(W("N1"), R(pz, 0, 128), W("TT"), AL.max)
-        tt(W("N2"), R(pu, 0, 128), W("N1"), AL.max)
-        xw = R("X", nw, nw + 2 * E)
-        act(W("OX"), IND(xw, vl), AF.Copy)
-        act(W("RG"), IND(W("RT"), cl), AF.Copy)
-        cp(W("G"), IND(W("NTB"), cl))
-        pb = bank()
-        mm(R(pb, 0, 128), [(M("Ih"), W("OX")), (M("Ih"), W("RG"))])
-        act(W("XN"), R(pb, 0, 128), AF.Identity, UP - UP * HALF, 1.0)
-        cp(IND(xw, vl), W("XN"))
-        pf = bank()
-        mm(R(pf, 0, 8), [(M("I"), W("CF"))] + sel("B14", "Z0", 0, 128))
-        ts(W("FL"), R(pf, 0, 8), 0.25, AL.add)
-        for w in range(6):
-            ts(R("U", w, E, 6), W("G"), 4 * w, AL.logical_shift_right, 15, AL.bitwise_and)
-        ts(R("X", O + S, O + S + E), W("U"), UP, AL.add)
-        cp(IND(R("X", O + S, O + S + E), W("FL")), W("OX"))
-
-        def finish(pb, col):
-            src, km, lk = R(pb, 0, 96), R("KM", col, col + 96), R("LK", col, col + 96)
+        mm(R(pu, 0, 128), [(M("I4k"), W("N4")), (M("L0"), old[0]), (M("L1"), old[1]), (M("nIq"), W("Z0"))])
+        if "t" in plan["scalar"]:
+            act(W("TT"), IND(W("QT"), cl), AF.Identity, float(S - E - 1024), 1.0)
+            mm(R(pv, 0, 128), [(M("BO"), R("CV", 128, 256)), (W("IF"), W("TT"))])
             if t == 0:
-                wr = R("WR", col - kc, col - kc + 96)
-                ts(wr, src, -1024.5, AL.is_lt, float(S), AL.mult)
-                tt(km, src, wr, AL.add)
-                src = km
-            ts(lk, src, 1024.25 + O, AL.add)
+                ts(W("VR"), R(pv, 0, 128), -1024.5, AL.is_lt, float(S), AL.mult)
+                tt(W("T2"), R(pv, 0, 128), W("VR"), AL.add)
+            else:
+                act(W("T2"), R(pv, 0, 128), AF.Copy)
+            back = W("T2")
+        else:
+            tt(W("TT"), IND(W("QT"), cl), W("VR"), AL.add)
+            back = W("TT")
+            if t == 0:
+                pw = bank()
+                ts(R(pw, 0, 128), W("TT"), -1024.5, AL.is_lt, float(S), AL.mult)
+                tt(W("T2"), R(pw, 0, 128), W("TT"), AL.add)
+                back = W("T2")
+        tt(W("N1"), R(pz, 0, 128), back, AL.max)
+        tt(W("N2"), R(pu, 0, 128), W("N1"), AL.max)
+        def spread(b, co, src):
+            us = (((0, ""), (1, ""), (2, "a")), ((2, "b"), (3, ""), (4, ""), (5, "c")), ((5, "d"), (6, ""), (7, "")))[co]
+            return [(M("K%d%s" % (b, x), 16 - (6 * u - 16 * co)), R(src, u, 128, 8)) for u, x in us]
 
+        cp(W("G"), IND(W("NTB"), cl))
+        for w in range(6):
+            ts(R("U", 128 * w + 128, 128 * w + 256), W("G"), 4 * w, AL.logical_shift_right, 15, AL.bitwise_and)
+        ts(W("N3"), W("Z0"), -12288.0 * 2048.0, AL.is_gt, cc(11), AL.mult)
+        pf = bank()
+        for co in range(3):
+            mm(R(pf, co, 48, 3), [(M("I"), R("KD", co, 48, 3))] + spread(0, co, "N3"))
+        ts(W("NL"), R(pf, 0, 48), -127.75, AL.add)
+        u = 0
+        for n in plan["nodes"]:
+            act(R("X", O + S + u, O + S + u + n), IND(W("U"), R("NL", u // 16, (u + n) // 16)), AF.Identity, UP, 1.0)
+            u += n
         pn = bank()
         for b in range(2):
-            for co, us in enumerate((((0, ""), (1, ""), (2, "a")), ((2, "b"), (3, ""), (4, ""), (5, "c")), ((5, "d"), (6, ""), (7, "")))):
-                mm(R(pn, 48 * b + co, 48 * b + 48, 3),
-                   [(M("K%d%s" % (b, x), 14 - (6 * u - 16 * co)), R("N2", u, 128, 8)) for u, x in us])
-        finish(pn, kc + 96)
+            for co in range(3):
+                mm(R(pn, 48 * b + co, 48 * b + 48, 3), spread(b, co, "N2"))
+        ts(R("LK", kc + 96, kc + 192), R(pn, 0, 96), 1024.25 + O, AL.add)
+        if t + 1 < RO:
+            for b in range(2):
+                act(R("KN", 112 + 56 * b, 160 + 56 * b), R(pn, 48 * b, 48 * b + 48), AF.Copy)
         p1, p2 = bank(), bank()
-        mm(R(p1, 0, 128), [(M("D01"), W("N2")), (M("A1"), W("N2"))])
+        step = [(M("L0"), old[0]), (M("L1"), old[1]), (M("nD"), W("N2")), (M("A3"), W("N2"))]
+        mm(R(p1, 0, 128), step)
+        mm(R(p2, 0, 128), step, True, False)
         act(W("HI"), R(p1, 0, 128), AF.Copy)
-        mm(R(p2, 0, 128), [(M("A1"), W("N2")), (M("A2"), W("HI"))])
-        act(R("NB", 8, 136), R(p2, 0, 128), AF.Copy)
-        act(W("RB"), IND(W("NB"), W("LS")), AF.Copy)
+        mm(R(p2, 0, 128), [(M("A3"), W("HI"))], False, True)
+        act(W("NB"), R(p2, 0, 128), AF.Copy)
+        dk = E * (RO - 1 - t)
+        cp(IND(R("DK", dk, dk + 2 * E), vl), W("NB"))
         pk = bank()
         for b in range(2):
-            mm(R(pk, 48 * b, 48 * b + 48), [(M("I"), R("KP", 48 * b, 48 * b + 48))] + sel("B%dr" % b, "RB", 0, E))
-        finish(pk, kc)
+            kn = 112 * t + 56 * b
+            mm(R(pk, 48 * b, 48 * b + 48), [(W("IF"), R("KN", kn, kn + 48))] + sel("B%dr" % b, "DK", dk, E))
+        ts(R("LK", kc, kc + 96), R(pk, 0, 96), 1024.25 + O, AL.add)
+        row[0] = "rest%d" % t
         stage2(0, S, plan["rest"][t], t)
+        row[0] = "next%d" % t
         stage1(0, S, plan["early"][t])
-        stage1(S, S + E, plan["late"][t][:len(plan["late"][t]) // 2])
-        stage1(S - E, S + E, plan["late"][t][len(plan["late"][t]) // 2:])
-    stage2(0, A, plan["last"], RO)
+        stage1(S, S + E, plan["lnew"][t])
+        stage1(S - E, S + E, plan["lold"][t])
+    row[0] = "last"
+    last(plan["last"])
     return ops
 
 
@@ -522,7 +629,7 @@ def depend(ops):
                     if ps and not same:
                         dep[k] = True
                     elif hit and (kind == "w" or kk == "w"):
-                        wait = (not same) or (kk == "w" and op["eng"] != "p")
+                        wait = (not same) or op["eng"] != "p"
                         dep[k] = dep.get(k, False) or wait
                     elif ps and op["eng"] == "p":
                         dep[k] = dep.get(k, False)
@@ -532,88 +639,261 @@ def depend(ops):
                 if kind == "w" and r[3] == 1 and not r[0].startswith("ps"):
                     h[:] = [e for e in h if not (r[1] <= e[2] and e[3] <= r[2])]
                 elif r[0].startswith("ps"):
-                    h[:] = h[-24:]
+                    h[:] = h[-40:]
                 h.append((n, kind, r[1], r[2]))
         op["dep"] = dep
     last = {}
     for n, op in enumerate(ops):
-        if op["kind"] in ("send", "load"):
-            if op["eng"] in last:
-                op["dep"].setdefault(last[op["eng"]], False)
-            last[op["eng"]] = n
+        row = op["kind"] in ("send", "load") or op.get("row")
+        if row:
+            if (op["eng"], row) in last:
+                op["dep"].setdefault(last[op["eng"], row], False)
+            last[op["eng"], row] = n
     for op in ops:
         if op["kind"] == "arrive":
             for n, o2 in enumerate(ops):
-                if o2["kind"] == "send" and (o2["args"][0] == "RT") == (op["sem"] == "rt_in"):
+                if o2["kind"] == "send" and o2["args"][0] == op["args"][0]:
                     op["dep"][n] = True
 
 
 def order(ops, C, plan):
     n = len(ops)
-    kids = [[] for _ in range(n)]
+    cost = [op["cost"] for op in ops]
+    eng = [op["eng"] for op in ops]
+    tail = [0.0 if op["kind"] == "send" else op["lat"] for op in ops]
+    early = [tail[k] + op["at"] for k, op in enumerate(ops)]
+    after = [[] for _ in range(n)]
+    before = [[] for _ in range(n)]
+    slow = [[] for _ in range(n)]
+    for c, op in enumerate(ops):
+        for k, wait in op["dep"].items():
+            gap = 0.0
+            if wait:
+                gap = ops[k]["lat"] + (C["same"] if eng[c] == eng[k] and "sem" not in ops[k] else C["hop"])
+            after[k].append((c, gap))
+            more = C["margin"] if wait and ops[k]["kind"] == "send" else 0.0
+            before[c].append((k, gap + more))
+            slow[k].append((c, gap + more))
+
+    uses = {}
     for k, op in enumerate(ops):
-        for d in op["dep"]:
-            kids[d].append(k)
+        for r in op["rd"] + op["wr"]:
+            if r[0].startswith("ps") and k not in uses.setdefault(r[0], []):
+                uses[r[0]].append(k)
+    opens = {ks[0]: name for name, ks in uses.items()}
+    inside = {k: name for name, ks in uses.items() for k in ks}
+    caps = dict(zip("ADLZ", plan["banks"]))
+
+    def lay(nexts, prevs, ready, way, banks):
+        left = [len(p) for p in prevs]
+        ready = list(ready)
+        free, pool, seq = {}, {}, {}
+        start = [0.0] * n
+        idle = {b: (0.0, None) for b in range(8)}
+        held, todo, place = {}, {name: len(ks) for name, ks in uses.items()}, {}
+        lists = sum(name[2] in "AL" for name in uses)
+        shut = {kind: [k for k, name in opens.items() if name[2] == kind] for kind in caps}
+
+        def due(k):
+            if not banks or k not in opens:
+                return ready[k]
+            kind = opens[k][2]
+            keep = (5 if lists else 2) if kind == "Z" else 0
+            ahead = sum(way[j] > way[k] for j in shut[kind])
+            if len(idle) <= keep or sum(name[2] == kind for name in held) + ahead >= caps[kind]:
+                return None
+            return max(ready[k], min(t for t, _ in idle.values()))
+
+        for k in range(n):
+            if left[k] == 0:
+                pool.setdefault(eng[k], []).append(k)
+        for _ in range(n):
+            best = None
+            for e, p in pool.items():
+                at = {k: due(k) for k in p}
+                at = {k: t for k, t in at.items() if t is not None}
+                if not at:
+                    continue
+                now = max(free.get(e, 0.0), min(at.values()))
+                k = max((k for k in at if at[k] <= now), key=lambda j: way[j])
+                for j in at:
+                    if at[j] > now and way[j] - way[k] > plan["patience"] and at[j] - now < plan["near" if e in "vs" else "wide"] * cost[k]:
+                        k = j
+                st = max(now, at[k])
+                if best is None or st < best[0]:
+                    best = (st, e, k)
+            st, e, k = best
+            pool[e].remove(k)
+            seq.setdefault(e, []).append(k)
+            free[e] = st + cost[k]
+            start[k] = st
+            if banks and k in inside:
+                name = inside[k]
+                if k in opens:
+                    b = min(idle, key=lambda j: idle[j][0])
+                    place[name] = (b, idle.pop(b)[1])
+                    held[name] = 0.0
+                    shut[name[2]].remove(k)
+                held[name] = max(held[name], free[e] + C["hop"])
+                todo[name] -= 1
+                if todo[name] == 0:
+                    idle[place[name][0]] = (held.pop(name), name)
+                    lists -= name[2] in "AL"
+            for c, gap in nexts[k]:
+                ready[c] = max(ready[c], free[e] + gap)
+                left[c] -= 1
+                if left[c] == 0:
+                    pool.setdefault(eng[c], []).append(c)
+        return seq, start, place
+
     way = [-1.0] * n
     todo = list(range(n - 1, -1, -1))
     while todo:
         rest = []
         for k in todo:
-            if any(way[c] < 0 for c in kids[k]):
+            if any(way[c] < 0 for c, _ in after[k]):
                 rest.append(k)
             else:
-                op = ops[k]
-                way[k] = op["cost"] + max([way[c] + (op["lat"] + C["hop"] if ops[c]["dep"][k] else 0.0) for c in kids[k]] + [op["lat"]])
+                way[k] = cost[k] + max([way[c] + gap for c, gap in slow[k]] + [early[k]])
         todo = rest
-    left = [len(op["dep"]) for op in ops]
-    ready = [op["at"] for op in ops]
-    free = {}
-    pool = {}
+    best = None
+    for _ in range(plan["turns"]):
+        seq, start, place = lay(after, before, [0.0] * n, way, True)
+        end = max(start[k] + cost[k] + tail[k] for k in range(n))
+        if best is None or end < best[1]:
+            best = (seq, end, start, place)
+        back = lay(before, after, early, [start[k] + cost[k] for k in range(n)], False)[1]
+        way = [back[k] + cost[k] for k in range(n)]
     for k in range(n):
-        if left[k] == 0:
-            pool.setdefault(ops[k]["eng"], []).append(k)
+        ops[k]["st"] = best[2][k]
+    for name, (b, was) in best[3].items():
+        for k in uses.get(was, []):
+            first = uses[name][0]
+            ops[first]["dep"][k] = ops[first]["dep"].get(k, False) or not (eng[k] == eng[first] == "p")
+    return best[0], best[1], {name: "ps%d" % b for name, (b, _) in best[3].items()}
+
+
+def order2(ops, C, plan):
+    n = len(ops)
+    cost = [op["cost"] for op in ops]
+    eng = [op["eng"] for op in ops]
+    tail = [0.0 if op["kind"] == "send" else op["lat"] for op in ops]
+    early = [tail[k] + op["at"] for k, op in enumerate(ops)]
+    after = [[] for _ in range(n)]
+    before = [[] for _ in range(n)]
+
+    def edge(k, c, wait):
+        gap = ops[k]["lat"] + (C["same"] if eng[c] == eng[k] and "sem" not in ops[k] else C["hop"]) if wait else 0.0
+        after[k].append((c, gap))
+        before[c].append((k, gap))
+
+    for c, op in enumerate(ops):
+        for k, wait in op["dep"].items():
+            edge(k, c, wait)
+    uses = {}
+    for k, op in enumerate(ops):
+        for r in op["rd"] + op["wr"]:
+            if r[0].startswith("ps") and k not in uses.setdefault(r[0], []):
+                uses[r[0]].append(k)
+
+    def lay(nexts, prevs, ready, way):
+        start = [0.0] * n
+        busy = {}
+        left = [len(p) for p in prevs]
+        pool = [k for k in range(n) if left[k] == 0]
+        while pool:
+            k = max(pool, key=lambda j: way[j])
+            pool.remove(k)
+            t = max([ready[k]] + [start[j] + cost[j] + gap for j, gap in prevs[k]])
+            line = busy.setdefault(eng[k], [])
+            i = 0
+            for a, b in line:
+                if t + cost[k] <= a:
+                    break
+                t = max(t, b)
+                i += 1
+            line.insert(i, (t, t + cost[k]))
+            start[k] = t
+            for c, _ in nexts[k]:
+                left[c] -= 1
+                if left[c] == 0:
+                    pool.append(c)
+        return start
+
+    def banks(start):
+        line = sorted((start[k], k) for k in range(n) if eng[k] == "p")
+        for name in sorted(uses, key=lambda m: -start[uses[m][0]]):
+            k = uses[name][0]
+            if eng[k] == "p":
+                t = min(start[c] - gap for c, gap in after[k]) - cost[k]
+                line.remove((start[k], k))
+                for a, j in reversed(line):
+                    if a + cost[j] <= t:
+                        break
+                    if a < t + cost[k]:
+                        t = a - cost[k]
+                start[k] = max(t, start[k])
+                line.append((start[k], k))
+                line.sort()
+        idle = {b: (0.0, None) for b in range(8)}
+        place = {}
+        for name in sorted(uses, key=lambda m: start[uses[m][0]]):
+            b = min(idle, key=lambda j: idle[j][0])
+            if idle[b][0] > start[uses[name][0]] + 1e-6:
+                return None, (name, [m for _, m in idle.values()])
+            place[name] = (b, idle[b][1])
+            idle[b] = (max(start[k] + cost[k] for k in uses[name]) + C["hop"], name)
+        return place, None
+
+    way = [0.0] * n
+    for k in sorted(range(n), key=lambda j: -lay(after, before, [0.0] * n, way)[j] if False else -j):
+        way[k] = cost[k] + max([way[c] + gap for c, gap in after[k]] + [early[k]])
+    for _ in range(3):
+        for k in range(n - 1, -1, -1):
+            way[k] = cost[k] + max([way[c] + gap for c, gap in after[k]] + [early[k]])
+    best = None
+    for turn in range(plan["turns"]):
+        while True:
+            start = lay(after, before, [0.0] * n, way)
+            place, clash = banks(start)
+            if clash is None:
+                break
+            name, held = clash
+            late = min(held + [name], key=lambda m: way[uses[m][0]])
+            done = min((m for m in held + [name] if m != late), key=lambda m: max(start[k] + cost[k] for k in uses[m]))
+            for k in uses[done]:
+                edge(k, uses[late][0], True)
+        end = max(start[k] + cost[k] + tail[k] for k in range(n))
+        if best is None or end < best[1]:
+            best = (start, end, place)
+        back = lay(before, after, early, [start[k] + cost[k] for k in range(n)])
+        way = [back[k] + cost[k] for k in range(n)]
     seq = {}
-    end = 0.0
-    for _ in range(n):
-        best = None
-        for e, p in pool.items():
-            if not p:
-                continue
-            now = max(free.get(e, 0.0), min(ready[k] for k in p))
-            k = max((k for k in p if ready[k] <= now), key=lambda j: way[j])
-            for j in p:
-                if ready[j] > now and way[j] - way[k] > plan["patience"] and ready[j] - now < plan["near"] * ops[k]["cost"]:
-                    k = j
-            st = max(now, ready[k])
-            if best is None or st < best[0]:
-                best = (st, e, k)
-        st, e, k = best
-        pool[e].remove(k)
-        seq.setdefault(e, []).append(k)
-        free[e] = st + ops[k]["cost"]
-        ops[k]["st"] = st
-        if ops[k]["kind"] != "send":
-            end = max(end, free[e] + ops[k]["lat"])
-        for c in kids[k]:
-            if ops[c]["dep"][k]:
-                same = ops[c]["eng"] == e and "sem" not in ops[k]
-                ready[c] = max(ready[c], free[e] + ops[k]["lat"] + (C["same"] if same else C["hop"]))
-            else:
-                ready[c] = max(ready[c], free[e])
-            left[c] -= 1
-            if left[c] == 0:
-                pool.setdefault(ops[c]["eng"], []).append(c)
-    return seq, end
+    for k in sorted(range(n), key=lambda j: (best[0][j], j)):
+        ops[k]["st"] = best[0][k]
+        seq.setdefault(eng[k], []).append(k)
+    for name, (b, was) in best[2].items():
+        for k in uses.get(was, []):
+            first = uses[name][0]
+            ops[first]["dep"][k] = ops[first]["dep"].get(k, False) or not (eng[k] == eng[first] == "p")
+    return seq, best[1], {name: "ps%d" % b for name, (b, _) in best[2].items()}
 
 
 def hands(T, topo, rank):
     me = T.cores[rank]
-    others = sorted((c for c in topo.cores_of(me) if c != me), key=lambda c: (topo.die(c) == topo.die(me), c))
-    n = len(T.cores)
-    dst = [(rank + 1 + j) % n for j in range(n - 1)]
-    pairs = [("NTB", d) for d in dst] + [("QT", d) for d in reversed(dst)]
-    mix = [0, 4, 1, 5, 2, 6, 3]
-    return {others[mix[j]]: pairs[2 * j:2 * j + 2] for j in range(n - 1)}
+    far = [c for c in topo.cores_of(me) if topo.die(c) != topo.die(me)]
+    near = [c for c in topo.cores_of(me) if topo.die(c) == topo.die(me) and c != me]
+    share = {"RT": ((me, 4), (far[2], 2), (far[3], 1)),
+             "QT": ((far[0], 2), (near[0], 2), (far[1], 2), (near[1], 1)),
+             "NTB": ((far[2], 2), (near[2], 2), (far[3], 1), (near[1], 2))}
+    out = {}
+    for turn, (name, parts) in enumerate(share.items()):
+        dst = [T.cores[(rank + 1 + (j + 2 * turn) % (len(T.cores) - 1)) % len(T.cores)] for j in range(len(T.cores) - 1)]
+        out[name] = []
+        for c, k in parts:
+            out[name].append((c, dst[:k]))
+            dst = dst[k:]
+    return out
 
 
 def bits(es):
@@ -628,20 +908,50 @@ def dst_id(topo, dst, src):
     return DstId(rid=rid, pnc=pid)
 
 
+def transfer(T, topo, core, name, rank, to, es, sem):
+    part = T[name][:, rank * NT:rank * NT + NT]
+    return RemoteDMATransfer(dst_ids=[dst_id(topo, c, core) for c in to], dma_engine_mask=bits(es), remote_sem=T.sem[sem + name],
+                             src=part, dsts=[part] * len(to))
+
+
+def folder(topo, me, j):
+    near = [c for c in topo.cores_of(me) if topo.die(c) == topo.die(me) and c != me]
+    return near[j % len(near)]
+
+
+LAID = {}
+
+
+def laid(rank):
+    if rank not in LAID:
+        ops = build(rank, COST, PLAN)
+        depend(ops)
+        seq, _, banks = order(ops, COST, PLAN)
+        LAID[rank] = (ops, seq, banks)
+    return LAID[rank]
+
+
 def helper(g, core, T, topo):
     for rank, me in enumerate(T.cores):
         if core in topo.cores_of(me):
-            pairs = hands(T, topo, rank)[core]
-            g.wait_ge(T.sem.hand_in, len(topo.engines(me, core)) * len(set(p[0] for p in pairs)))
-            trs = []
             used = 0
-            for j, (name, d) in enumerate(pairs):
-                es = topo.engines(core, T.cores[d])
-                h = len(es) // 2
-                used += h
-                trs.append(RemoteDMATransfer(dst_ids=[dst_id(topo, T.cores[d], core)], dma_engine_mask=bits(es[j * h:j * h + h]),
-                                             remote_sem=T.sem.tab_in, src=T[name][:, 0:NT], dst=T[name][:, rank * NT:rank * NT + NT]))
-            g.remote_dma_fused(trs, local_sem=T.sem.sent)
+            for name, parts in hands(T, topo, rank).items():
+                for c, to in parts:
+                    if c == core:
+                        es = topo.engines(core, to[0])
+                        g.wait_ge(T.sem["hand_" + name], len(es))
+                        g.remote_dma_fused([transfer(T, topo, core, name, rank, to, es, "in_")], local_sem=T.sem.sent)
+                        used += len(es)
+            ops, seq, _ = laid(rank)
+            es = topo.engines(core, me)
+            for k in seq["g"]:
+                if ops[k]["kind"] == "fold" and folder(topo, me, ops[k]["args"][2]) == core:
+                    name, a, b, _ = ops[k]["args"][0]
+                    j = ops[k]["args"][2]
+                    g.wait_ge(T.sem["fold%d" % j], len(es))
+                    rid, pid = topo.addr(me, core)
+                    g.remote_dma(T[name][:, a:b], T[name][:, a:b], T.sem["back%d" % j], T.sem.sent, pid, rid, bits(es))
+                    used += len(es)
             g.wait_ge(T.sem.sent, used)
 
 
@@ -650,20 +960,20 @@ def rank_program(g, core, T, topo):
     if rank is None:
         helper(g, core, T, topo)
         return
-    ops = build(rank, COST, PLAN)
-    depend(ops)
-    seq, _ = order(ops, COST, PLAN)
+    ops, seq, banks = laid(rank)
     Q = {"v": g.vector, "s": g.scalar, "p": g.tensor, "g": g, "y": g.sync}
-    plan = hands(T, topo, rank)
+    handed = hands(T, topo, rank)
     peers = [c for c in T.cores if c != core]
     off = topo.engines(core, peers[0])
+    spare = [e for e in topo.engines(core, handed["NTB"][0][0]) if e not in off]
 
     def ap(r):
         if not isinstance(r, tuple):
             return r
         if r[0] == "@":
             return ap(r[1]).indirect(ap(r[2]))
-        return T[r[0]][:, r[1]:r[2]:r[3]] if r[3] != 1 else T[r[0]][:, r[1]:r[2]]
+        buf = T[banks.get(r[0], r[0])]
+        return buf[:, r[1]:r[2]:r[3]] if r[3] != 1 else buf[:, r[1]:r[2]]
 
     needed = set()
     for op in ops:
@@ -692,18 +1002,14 @@ def rank_program(g, core, T, topo):
     sent = [0]
 
     def send(name):
-        src = T[name][:, rank * NT:rank * NT + NT]
-        if name == "RT":
-            es = off
-            tr = RemoteDMATransfer(dst_ids=[dst_id(topo, c, core) for c in peers], dma_engine_mask=bits(es), remote_sem=T.sem.rt_in,
-                                   src=src, dsts=[src] * len(peers))
+        cores = [c for c, _ in handed[name] if c != core]
+        direct = [to for c, to in handed[name] if c == core]
+        if direct:
+            trs = [transfer(T, topo, core, name, rank, direct[0], off, "in_"), transfer(T, topo, core, name, rank, cores, spare, "hand_")]
         else:
-            to = [c for c, pairs in plan.items() if name in [p[0] for p in pairs]]
-            es = topo.engines(core, to[0])
-            tr = RemoteDMATransfer(dst_ids=[dst_id(topo, c, core) for c in to], dma_engine_mask=bits(es), remote_sem=T.sem.hand_in,
-                                   src=src, dsts=[T[name][:, 0:NT]] * len(to))
-        g.remote_dma_fused([tr], local_sem=T.sem.sent)
-        sent[0] += len(es)
+            trs = [transfer(T, topo, core, name, rank, cores[1::2], off, "hand_"), transfer(T, topo, core, name, rank, cores[::2], spare, "hand_")]
+        g.remote_dma_fused(trs, local_sem=T.sem.sent)
+        sent[0] += len(off) + len(spare)
 
     for e, ks in seq.items():
         if e == "x":
@@ -724,7 +1030,13 @@ def rank_program(g, core, T, topo):
             a = op["args"]
             kind = op["kind"]
             if kind == "send":
-                send(a[0])
+                send(*a)
+                continue
+            if kind == "fold":
+                tr = RemoteDMATransfer(dst_ids=[dst_id(topo, folder(topo, core, a[2]), core)], dma_engine_mask=bits(off + spare),
+                                       remote_sem=T.sem["fold%d" % a[2]], srcs=[ap(r) for r in a[1]], dsts=[ap(a[0])], alu_op=2)
+                g.remote_dma_fused([tr], local_sem=T.sem.sent)
+                sent[0] += len(off + spare)
                 continue
             if kind == "load":
                 q.dma_start(ap(a[0]), T[a[1][0]][:]).then_inc(T.sem[op["sem"]], 16)
@@ -753,6 +1065,8 @@ def rank_program(g, core, T, topo):
             elif kind == "mm":
                 for j, (l, r) in enumerate(a[1]):
                     ins = q.matmul(ap(a[0]), ap(l), ap(r), a[2] and j == 0, a[3] and j == len(a[1]) - 1)
+            elif kind == "sel":
+                ins = q.affine_select(ap(a[0]), ap(a[1]), a[2], a[3], a[4], a[5], a[6])
             elif SCRATCH[a[0][0]][2] == I32:
                 ins = q.iota(ap(a[0]), a[1], a[2], a[3])
             else:

from concourse.bass import DstId, RemoteDMATransfer
from concourse.mybir import AluOpType, ActivationFunctionType

AL = AluOpType
AF = ActivationFunctionType
V0, NT, E, A, RO = 1536, 256, 768, 3072, 2
O = 16
UP = 160.0
CR = 12582912.0
HALF = 31.0 / 64.0
MW = 160
MATS = ["I", "nI", "Ih", "I16", "I256", "I4k", "I64k", "I1m", "Iq", "nIq", "IB", "B1", "BW", "B0r", "B1r", "BO", "BO14",
        "nBO", "nBO6", "nBOk", "DI", "IW0", "IW1", "nD", "A3", "nU", "L0", "L1",
        "K0", "K1", "K0a", "K0b", "K0c", "K0d", "K1a", "K1b", "K1c", "K1d"]
BF, H16, F32, I32, U16 = "bfloat16", "float16", "float32", "int32", "uint16"
SB = {
    "X": (O + A, BF), "P": (O + A, BF), "RT": (2064, BF), "QT": (2056, F32), "NTB": (2056, F32), "NX": (V0, BF),
    "G": (128, I32), "U": (896, I32), "KD": (48, BF),
    "TK": (256, I32), "KIN": (192, I32), "WT": (4, I32), "TH": (4, I32), "WB": (8, BF),
    "KM": (96, F32), "KN": (224, F32), "LK": (384, U16), "KA": (192, F32), "KB": (192, F32),
    "MAT": (MW * len(MATS), BF), "IF": (128, F32), "CC": (48, F32), "CI": (8, I32), "IO": (MW, BF), "IOA": (128, BF),
    "IOB": (128, BF), "KI": (128, BF), "VT": (400, F32), "DC": (48, BF), "M50": (400, BF), "C50": (400, F32),
    "CZ": (256, H16), "N4": (128, BF), "AT": (144, BF),
    "DD": (256, H16), "CQ": (256, BF), "P0": (256, BF), "PF": (256, F32),
    "TA": (3072, BF), "TB": (3072, BF), "TC": (3072, BF), "TR": (3072, BF), "TD": (3072, BF), "TE": (3072, BF),
    "HM": (144, I32), "HC": (144, I32), "HD": (144, I32), "PO": (144, I32), "CL": (144, U16),
    "DF": (2304, BF), "AB": (2304, BF), "SG": (144, BF), "SC": (144, F32), "NR": (48, F32), "M01": (48, F32),
    "MX": (48, I32), "CT": (56, I32), "KEY": (48, I32), "IB": (400, BF), "S1": (400, BF),
    "S2": (400, F32), "RM": (400, BF), "L1": (8, U16), "L2F": (8, F32), "L2": (8, U16),
    "EE": (128, BF), "CV": (256, H16), "KE": (256, H16), "SL": (16, U16), "NL": (48, U16),
    "Z0": (128, BF), "OH": (128, BF), "RG": (128, BF),
    "VR": (128, F32), "TT": (128, F32), "T2": (128, F32), "N1": (128, F32), "N2": (128, H16), "N3": (128, BF),
    "DEAD": (48, BF), "WW": (3072, BF), "ONE": (400, BF), "HI": (128, BF), "NB": (128, BF), "DK": (2304, BF),
}
SCRATCH = {name: ("sbuf", [128, n], dtype) for name, (n, dtype) in SB.items()}
for _b in range(8):
    SCRATCH["ps%d" % _b] = ("psum", [128, 512], F32)
WIDTH = {BF: 2, H16: 2, U16: 2, F32: 4, I32: 4}
NDMA = 24
SEMAPHORES = ["sv", "ss", "sp", "sg", "in_RT", "in_NTB", "in_QT", "hand_RT", "hand_NTB", "hand_QT", "sent"] + ["d%d" % i for i in range(NDMA)]
SEMAPHORES += ["%s%d" % (nm, i) for nm in ("fold", "back") for i in range(12)]
ESEM = {"v": "sv", "s": "ss", "p": "sp", "g": "sg"}

COST = {"cyc": 1.04, "gat": 1.55, "sca": 3.8, "pe": 0.55, "vfix": 15.0, "sfix": 40.0, "hop": 120.0, "same": 60.0,
        "RT": 7500.0, "NTB": 11000.0, "QT": 11000.0, "margin": 4000.0, "dma": 1800.0, "rate": 250.0,
        "call": 1000.0, "fold": 4500.0, "foldcol": 1.0}
PLAN = {
    "first": [(64, "o"), (128, "v"), (256, "v"), (512, "v"), (320, "v"), (256, "v")],
    "new": [[(128, "O"), (256, "w"), (256, "w"), (128, "w")], [(192, "O"), (128, "m"), (192, "w"), (256, "w")]],
    "rest": [[(256, "m"), (128, "m"), (128, "s"), (256, "s")],
             [(64, "m"), (128, "s"), (128, "m"), (128, "m"), (192, "m")] + [(128, "m")] * 6 + [(128, "v")]],
    "early": [[(256, "v"), (128, "v"), (384, "v")], [(448, "v"), (320, "v"), (384, "v"), (256, "v"), (128, "v")]],
    "lnew": [[(256, "v"), (192, "v"), (320, "v")], [(384, "v")] * 2],
    "lold": [[(256, "v")] * 3, [(384, "v")] * 2],
    "last": [(256, "o"), (512, "v"), (512, "v"), (384, "v"), (384, "v"), (256, "v"), (384, "v"), (256, "v"), (128, "v")],
    "banks": [3, 2, 3, 6],
    "parts": [768],
    "dist": [[[(384, "v"), (384, "v")], [(384, "s"), (384, "v")], [(384, "v"), (256, "v"), (128, "v")]],
             [[(256, "v")] * 3, [(448, "s"), (320, "v")], [(448, "v"), (128, "v"), (192, "v")]]],
    "nodes": [384, 384],
    "patience": 1000.0, "near": 0.7, "wide": 3.0, "ahead": True, "scalar": "bpc", "turns": 3, "pace": 2.7, "sends": ["QT", "NTB"],
}


def R(name, a, b, step=1):
    return (name, a, b, step)


def W(name):
    return (name, 0, SCRATCH[name][1][1], 1)


def IND(win, off):
    return ("@", win, off)


def M(name, a=0, n=128):
    k = MATS.index(name) * MW
    return ("MAT", k + a, k + a + n, 1)


def KL(name, b, u, w):
    k = 96 * (u // E) + 48 * b + (u % E) // 16
    return (name, k, k + (w - u) // 16, 1)


def ncols(r):
    if r[0] == "@":
        return 16 * ncols(r[2])
    return (r[2] - r[1] + r[3] - 1) // r[3]


def regs(r):
    if not isinstance(r, tuple):
        return []
    if r[0] == "@":
        return [r[1], r[2]]
    return [r]


def two_bytes(rs):
    return all(r[0] in SB and WIDTH[SB[r[0]][1]] == 2 for r in rs)


def cut(u, w):
    out = []
    while u < w:
        e = min(w, (u // E + 1) * E)
        out.append((u, e))
        u = e
    return out


def build(rank, C, plan):
    ops = []
    row = [None]

    def add(eng, kind, args, out, ins, cost, **kw):
        rd, wr = [], []
        for r in ins:
            rd += regs(r)
        for r in out:
            if r[0] == "@":
                wr.append(r[1]); rd.append(r[2])
            else:
                wr.append(r)
        d = {"eng": eng, "kind": kind, "args": args, "rd": rd, "wr": wr, "cost": cost, "lat": 0.0, "at": 0.0}
        d.update(kw)
        if row[0] and any(isinstance(r, tuple) and r[0] == "@" and r[2][0] in ("LK", "CL") for r in ins):
            d["row"] = row[0]
        if out and out[0][0] == "AB":
            d["row"] = row[0] + "abs"
        ops.append(d)

    def vcost(out, in0, full):
        n = ncols(out)
        if out[0] == "@":
            return 50.0 + n * C["sca"] * C["cyc"]
        if in0[0] == "@":
            return 50.0 + n * C["gat"] * C["cyc"]
        return C["vfix"] + max(64.0, n * full) * C["cyc"]

    def ts(out, in0, s1, op0, s2=None, op1=None):
        f = 0.5 if in0[0] != "@" and two_bytes([out, in0]) else 1.0
        add("v", "ts", (out, in0, s1, s2, op0, op1), [out], [in0, s1, s2], vcost(out, in0, f))

    def tt(out, in0, in1, op):
        f = 1.0 if in0[0].startswith("ps") or in1[0].startswith("ps") else 2.0
        add("v", "tt", (out, in0, in1, op), [out], [in0, in1], vcost(out, in0, f))

    def cp(out, in0):
        f = 0.5 if in0[0] != "@" and out[0] != "@" and two_bytes([out, in0]) else 1.0
        add("v", "cp", (out, in0), [out], [in0], vcost(out, in0, f))

    def scan(out, d0, d1, op0, op1):
        f = 0.5 if two_bytes([out, d0, d1]) else 1.0
        add("v", "scan", (out, d0, d1, 0.0, op0, op1), [out], [d0, d1], vcost(out, d0, f))

    def ms(out, val):
        add("v", "ms", (out, val), [out], [], vcost(out, out, 0.5 if two_bytes([out]) else 1.0))

    def act(out, in0, func, bias=0.0, scale=1.0):
        c = 65.0 + ncols(out) * C["gat"] * C["cyc"] if in0[0] == "@" else C["sfix"] + max(64, ncols(out)) * C["cyc"]
        add("s", "act", (out, in0, func, bias, scale), [out], [in0, bias, scale], c)

    def mm(out, pairs, start=True, stop=True):
        ins = [] if start else [out]
        c = 30.0
        for l, r in pairs:
            ins += [l, r]
            c += max(64, ncols(out)) * C["pe"] * (1 if two_bytes([l]) else 4)
        add("p", "mm", (out, pairs, start, stop), [out], ins, c)

    def iota(out, pattern, base, mult=0):
        add("g", "iota", (out, pattern, base, mult), [out], [], 130.0 + 2 * ncols(out) * C["cyc"])

    def keep(out, in0, pattern, base, mult=0):
        add("g", "sel", (out, in0, pattern, AL.is_ge, 0.0, base, mult), [out], [in0], 170.0 + 2 * ncols(out) * C["cyc"])

    def fill(out, val):
        iota(out, [[0, ncols(out)]], val)

    def aff(out, in0, scale, bias):
        if "c" in plan["scalar"]:
            act(out, in0, AF.Identity, bias, scale)
        else:
            ts(out, in0, scale, AL.mult, bias, AL.add)

    def mat(kind, name, n, src, col, base, scale):
        if kind in plan["scalar"]:
            act(M(name, 0, n), M(base, 0, n), AF.Copy, 0.0, scale)
        else:
            ts(M(name, 0, n), src, col, AL.is_equal, scale, AL.mult)

    nd = [0, 0, 0, 0]

    def bank(kind="L"):
        nd[2] += 1
        return "ps%s%d" % (kind, nd[2])

    def dma(q, kind, sb, dr, nbytes):
        if kind == "load":
            nd[1] += nbytes
            add(q, kind, (sb, dr), [sb], [], 60.0, lat=C["dma"] + nd[1] / C["rate"], sem="d%d" % nd[0])
        else:
            add(q, kind, (sb, dr), [], [sb], 60.0 + nbytes / C["rate"], lat=C["dma"], sem="d%d" % nd[0])
        nd[0] += 1

    own = rank * NT
    cc = lambda j: R("CC", j, j + 1)
    dma("s", "load", R("RT", own, own + NT), ("rx",), 65536)
    dma("s", "load", R("KIN", 0, 96), ("k0",), 49152)
    dma("s", "load", R("KIN", 96, 192), ("k1",), 49152)
    dma("y", "load", R("X", O, O + V0), ("x0",), 393216)
    dma("s", "load", R("WT", 0, 1), ("wt",), 8192)
    dma("s", "load", R("TH", 0, 1), ("th",), 8192)
    dma("y", "load", W("TK"), ("tk",), 131072)
    dma("y", "load", W("NX"), ("nx",), 393216)
    iota(R("CI", 0, 1), [[0, 1]], 0, 1)
    iota(W("IO"), [[1, MW]], 0)
    iota(W("IOA"), [[16, 8], [0, 16]], 0)
    iota(W("IOB"), [[16, 8], [0, 8], [128, 2]], 0)
    add("g", "send", ("RT",), [], [R("RT", own, own + NT)], 1500.0, lat=C["RT"])
    for o in range(8):
        if o != rank:
            for nm in ("RT", "NTB", "QT"):
                add("x", "arrive", (nm,), [R(nm, o * NT, o * NT + NT)], [], 0.0, sem="in_" + nm)
    ms(R("X", 0, O), 0.0); ms(R("P", 0, O), 0.0); ms(W("KN"), -4096.0)
    ts(W("KA"), W("KIN"), -1024.0, AL.add)
    ts(W("KB"), W("KIN"), -8.0, AL.mult, 20480.0, AL.add)
    for b in range(2):
        for j, out in enumerate((R("KM", 48 * b, 48 * b + 48), R("KN", 56 * b, 56 * b + 48))):
            k = 96 * b + 48 * j
            tt(out, R("KA", k, k + 48), R("KB", k, k + 48), AL.min)
        ts(R("LK", 96 + 48 * b, 144 + 48 * b), R("KN", 56 * b, 56 * b + 48), 1024.25 + O, AL.add)
    ts(R("LK", 0, 96), W("KM"), 1024.25 + O, AL.add)
    ts(R("CI", 1, 2), R("CI", 0, 1), 15, AL.bitwise_and)
    ts(R("CI", 2, 3), R("CI", 0, 1), 1, AL.logical_shift_right, 7, AL.bitwise_and)
    ts(R("CI", 3, 4), R("CI", 0, 1), 1, AL.bitwise_and)
    cp(R("CC", 0, 4), R("CI", 0, 4))
    io = R("IO", 0, 128)
    ts(M("I"), io, cc(0), AL.is_equal)
    for nm, sc in (("nI", -1.0), ("Ih", HALF), ("IW0", UP - 1.0), ("IW1", UP - 2 * UP * HALF - 1.0), ("I256", 256.0),
                   ("I16", 16.0), ("I4k", 4096.0), ("I64k", 65536.0), ("I1m", 1048576.0), ("Iq", 1.0 / 2048.0), ("nIq", -1.0 / 2048.0), ("IB", 5120.0)):
        mat("i", nm, 128, io, cc(0), "I", sc)
    act(W("IF"), M("I"), AF.Copy)
    tt(cc(4), cc(0), cc(1), AL.subtract)
    aff(cc(5), cc(4), 1.0, 15.0)
    aff(cc(7), cc(2), 1.0, -16.0)
    ts(cc(8), cc(1), 14.0, AL.is_equal)
    io3 = R("IO", 0, 143)
    ts(M("B1", 0, 143), io3, cc(5), AL.is_equal)
    ts(M("BO"), W("IOA"), cc(4), AL.is_equal)
    mat("b", "BO14", 128, W("IOA"), cc(4), "BO", cc(8))
    ms(W("ONE"), 1.0)
    for nm, sc in (("nBO", -1.0), ("nBO6", -6.0), ("nBOk", -1024.0)):
        mat("b", nm, 128, W("IOA"), cc(4), "BO", sc)
    ts(W("CQ"), W("TK"), 6.0, AL.min, -16.0, AL.add)
    ts(W("DD"), W("TK"), -6.0, AL.add, 0.0, AL.max)
    if "p" in plan["scalar"]:
        act(W("P0"), W("CQ"), AF.Relu, -15.0 * 8192.0, -8192.0)
    else:
        ts(W("P0"), W("CQ"), -16.0, AL.is_equal, 8192.0, AL.mult)
    p1, p2 = R(bank(), 0, NT), R(bank(), 0, NT)
    mm(p1, [(M("BO14"), W("CQ"))])
    mm(p2, [(M("Iq"), W("CQ")), (M("nI"), W("DD")), (M("nI"), W("P0"))])
    ts(W("PF"), p1, cc(7), AL.is_equal, -16384.0, AL.mult)
    tt(R("QT", own, own + NT), p2, W("PF"), AL.min)
    p1 = R(bank(), 0, NT)
    mm(p1, [(M(n), R("NX", w * NT, w * NT + NT)) for w, n in enumerate(("I", "I16", "I256", "I4k", "I64k", "I1m"))])
    act(R("NTB", own, own + NT), p1, AF.Copy)
    for nm in plan["sends"]:
        add("g", "send", (nm,), [], [R(nm, own, own + NT)], 1000.0, lat=C[nm])
    cp(cc(9), R("WT", 0, 1)); ts(cc(10), R("TH", 0, 1), -0.5, AL.add); cp(R("WB", 0, 1), R("WT", 0, 1))
    mat("b", "BW", 143, io3, cc(5), "B1", cc(9))
    p1 = R(bank(), 0, 1)
    mm(p1, [(M("BO"), R("WB", 0, 1))])
    act(cc(24), p1, AF.Copy, 0.0, -UP)
    keep(M("nU"), M("nBO"), [[-1, 128]], -1, 1)
    fill(W("N4"), -4)
    fill(R("RT", 2048, 2064), 0)
    keep(W("M50"), R("ONE", 0, 400), [[0, 8], [1, 50]], -1); fill(R("IB", 0, 400, 50), 0); fill(R("IB", 49, 400, 50), 1)
    u = 0
    for n in plan["parts"]:
        iota(R("AT", 3 * u // 16, 3 * (u + n) // 16), [[-4096, 3], [0, n // 16]], 5120)
        u += n
    iota(W("KI"), [[0, 8], [1, 16]], 1)
    iota(W("VT"), [[0, 8], [16, 50]], -16)
    fill(R("CT", 48, 56), 2048); fill(R("QT", 2048, 2056), -16384); fill(R("NTB", 2048, 2056), 0)
    for j in range(4):
        fill(R("X", O + V0 + 384 * j, O + V0 + 384 * j + 384), int(UP))
    for j in range(6):
        fill(R("DK", 384 * j, 384 * j + 384), 0)
    iota(W("DC"), [[0, 8], [16, 6]], 0)
    aff(cc(6), cc(4), 1.0, 128.0)
    aff(cc(12), cc(1), -6.0, 858.0)
    aff(cc(25), cc(1), 1024.0, 512.0)
    aff(cc(11), cc(2), 128.0, 0.0)
    for b, col in ((0, 4), (1, 6)):
        ts(M("L%d" % b), W("IOB"), cc(col), AL.is_equal)
    act(W("VT"), W("VT"), AF.Identity, cc(1), 1.0)
    act(R("VT", 49, 400, 50), R("IO", 0, 8), AF.Identity, cc(12), 96.0)
    act(W("DC"), W("DC"), AF.Identity, cc(1), 1.0)
    act(W("KD"), R("VT", 1, 49), AF.Identity, 128.0 - 5.0 / 12.0, 1.0 / 6.0)
    iota(W("C50"), [[1, 400]], 0)
    ts(M("DI"), io, cc(0), AL.is_equal, cc(25), AL.mult)
    for t in range(RO):
        ts(R("CZ", 128 * t, 128 * t + 128), io, 6.0, AL.mult, float(V0 + E * t - 1024), AL.add)
    ts(cc(13), cc(2), 1.0, AL.max, 6.0, AL.min)
    aff(cc(14), cc(2), 501.0, cc(5))
    aff(cc(15), cc(13), -500.0, cc(14))
    aff(cc(16), cc(3), 1000.0, 0.0)
    aff(cc(17), cc(3), -1000.0, 1000.0)
    aff(cc(26), cc(16), 1.0, cc(15))
    aff(cc(27), cc(17), 1.0, cc(15))
    ts(R("CC", 32, 34), R("IO", 2, 5, 2), cc(1), AL.is_gt, -1.0, AL.mult)
    ts(cc(23), cc(33), cc(3), AL.mult)
    aff(cc(22), cc(23), -1.0, cc(33))
    aff(cc(31), cc(0), 1.0, 2.0)
    ts(M("A3"), io, cc(31), AL.is_equal, cc(32), AL.mult)
    ts(M("nD"), io, cc(0), AL.is_equal, cc(32), AL.mult)
    for b in range(2):
        ts(M("K%d" % b, 0, MW), W("IO"), cc(26 + b), AL.is_equal)
        for x, step, base in (("a", -1, 3), ("b", 1, -4), ("c", -1, 1), ("d", 1, -2)):
            keep(M("K%d%s" % (b, x), 0, MW), M("K%d" % b, 0, MW), [[0, MW // 16], [step, 16]], base)
        mat("b", "B%dr" % b, 143, io3, cc(5), "B1", cc(22 + b))

    def sums(n, kind="A"):
        return R(bank(kind), 0, n)

    def diffs(n):
        return R(bank("D"), 0, n)

    def pair(table, S, u, w, first, out, alone):
        for a, b in cut(u, w):
            f = R(first[0], first[1] + a - u, first[1] + b - u)
            g0, g1 = (IND(R(table, 0, O + S), KL("LK", k, a, b)) for k in range(2))
            if alone:
                cp(f, g0)
            else:
                act(f, g0, AF.Copy)
            tt(R(out[0], out[1] + a - u, out[1] + b - u), g1, f, AL.max)

    def folded(table, S, u, w, names, less, more, out, both):
        for a, b in cut(u, w):
            for k, nm in enumerate(names):
                gk = IND(R(table, 0, O + S), KL("LK", k, a, b))
                if k == 0 or both:
                    act(R(nm, a, b), gk, AF.Identity, -less, 1.0)
                else:
                    ts(R(nm, a, b), gk, -less, AL.add)
        srcs = [R(nm, u, w) for nm in names] + more
        add("g", "fold", (out, srcs, nd[3]), [out], srcs, C["call"], lat=C["fold"] + (w - u) * C["foldcol"] * (len(srcs) + 1),
            sem="back%d" % nd[3])
        nd[3] += 1

    def stage1(u, S, pieces):
        for n, how in pieces:
            w = u + n
            ta, pp = R("TA", u, w), R("P", O + u, O + w)
            if how == "f":
                folded("X", S, u, w, ("TA", "TD"), 0.0, [], pp, True)
            elif how != "s":
                pair("X", S, u, w, ta, pp, how == "o")
            else:
                g0, g1 = (IND(R("X", 0, O + S), KL("LK", b, u, w)) for b in range(2))
                td, te = R("TD", u, w), R("TE", u, w)
                pd, pa = diffs(n), sums(n)
                act(ta, g0, AF.Copy)
                act(td, g1, AF.Copy)
                mm(pd, [(M("nI"), ta), (M("I"), td)])
                act(te, pd, AF.Relu)
                mm(pa, [(M("I"), ta), (M("I"), te)])
                act(pp, pa, AF.Copy)
            u = w

    def stage2(u, S, pieces, sweep):
        for n, how in pieces:
            w = u + n
            tb, tc, tr = (R(nm, u, w) for nm in ("TB", "TC", "TR"))
            pd, pa = diffs(n), sums(n)
            xs, pp = R("X", O + u, O + w), R("P", O + u, O + w)
            lift = UP if sweep == 0 else UP - 2 * UP * HALF
            if how in "fg":
                folded("P", S, u, w, ("TB", "TC"), 2.0, [pp], tr, how == "f")
                for a in range(u, w, 512):
                    b = min(w, a + 512)
                    pa = sums(b - a)
                    mm(pa, [(M("Ih"), R("X", O + a, O + b)), (M("Ih"), R("TR", a, b))])
                    act(R("X", O + a, O + b), pa, AF.Identity, lift, 1.0)
                u = w
                continue
            if how in "wO":
                ww = R("WW", u, w)
                mm(pd, [(M("Ih"), xs), (M("Ih"), pp)])
                act(ww, pd, AF.Identity, lift, 1.0)
                mm(pa, [(M("IW%d" % sweep), R("ONE", 0, n)), (M("Ih"), xs)], True, False)
                pair("P", S, u, w, tb, tc, how == "O")
                mm(pa, [(M("Ih"), tc)], False, True)
                tt(xs, pa, ww, AL.max)
                u = w
                continue
            mm(pa, [(M("Ih"), xs), (M("Ih"), pp)], True, False)
            if how == "s":
                g0, g1 = (IND(R("P", 0, O + S), KL("LK", b, u, w)) for b in range(2))
                te = R("TE", u, w)
                act(tb, g0, AF.Copy)
                act(tc, g1, AF.Copy)
                mm(pd, [(M("nI"), tb), (M("I"), tc)])
                act(te, pd, AF.Relu)
                mm(pd, [(M("nI"), pp), (M("I"), tb), (M("I"), te)])
            else:
                pair("P", S, u, w, tb, tc, how == "o")
                mm(pd, [(M("nI"), pp), (M("I"), tc)])
            act(tr, pd, AF.Relu, -2.0, 1.0)
            mm(pa, [(M("Ih"), tr)], False, True)
            if how in "vo":
                ts(xs, pa, lift, AL.add)
            else:
                act(xs, pa, AF.Identity, lift, 1.0)
            u = w

    def last(pieces):
        w = 0
        for j, (n, how) in enumerate(pieces):
            u, w = w, w + n
            tb, tc, tr = (R(nm, u, w) for nm in ("TB", "TC", "TR"))
            pa, pd = sums(n, "Z"), diffs(n)
            xs, pp = R("X", O + u, O + w), R("P", O + u, O + w)
            if how in "fg":
                folded("P", A, u, w, ("TB", "TC"), 2.0, [pp], tr, how == "f")
                mm(pa, [(M("Ih"), xs), (M("Ih"), tr)])
            else:
                mm(pa, [(M("Ih"), xs), (M("Ih"), pp)], True, False)
                mm(pd, [(M("nI"), pp)], True, False)
                pair("P", A, u, w, tb, tc, how == "o")
                mm(pd, [(M("I"), tc)], False, True)
                act(tr, pd, AF.Relu, -2.0, 1.0)
                mm(pa, [(M("Ih"), tr)], False, True)
            ts(xs, pa, CR, AL.add, -CR - 2 * UP * HALF, AL.add)
            dma("y", "store", xs, ("y", u, w), 256 * n)
            ops[-1]["at"] = (A - w) * plan["pace"]

    def sel(base, src, a, n):
        return [(M(base, 15 - r), R(src, a + r, a + n, 16)) for r in range(16)]

    row[0] = "first"
    stage1(0, V0, plan["first"])
    fill(R("X", 0, O), int(UP))
    for t in range(RO):
        S = V0 + E * t
        nw = O + S - E
        kc = 96 * (t + 1)
        row[0] = "new%d" % t
        stage2(S - E, S, plan["new"][t], t)
        u = 0
        row[0] = "far%d" % t
        for h, n in enumerate(plan["parts"]):
            c, k = u // 16, n // 16
            at = lambda nm, a, b: R(nm, 3 * c + a * k, 3 * c + b * k)
            pb = bank()
            mm(R(pb, 0, k), sel("BW", "X", nw + u, n))
            for m in range(3):
                ts(at("HM", m, m + 1), R(pb, 0, k), cc(24), AL.add, float(97 * m + 31 * t), AL.add)
            for a, b in ((0, 1), (1, 3)) if plan["ahead"] else ((0, 3),):
                ts(at("HC", a, b), at("HM", a, b), 2047, AL.bitwise_and)
                ts(at("HD", a, b), at("HC", a, b), 2049.0, AL.mult)
                ts(at("PO", a, b), at("HD", a, b), 3, AL.logical_shift_right, 2047, AL.bitwise_and)
                cp(at("CL", a, b), at("PO", a, b))
            pb, pl = bank(), bank()
            end = u + n == E
            for m in range(3):
                a = 0
                for w, how in plan["dist"][t][3 * h + m]:
                    gr = IND(W("RT"), R("CL", 3 * c + m * k + a // 16, 3 * c + m * k + (a + w) // 16))
                    d = E * m + u + a
                    xs, df, ab = R("X", nw + u + a, nw + u + a + w), R("DF", d, d + w), R("AB", d, d + w)
                    if how == "v":
                        tt(df, gr, xs, AL.subtract)
                        act(ab, df, AF.Abs, UP, 1.0)
                    else:
                        pd = diffs(w)
                        act(df, gr, AF.Copy)
                        mm(pd, [(M("nI"), xs), (M("I"), df)])
                        act(ab, pd, AF.Abs, UP, 1.0)
                    a += w
                mm(R(pl, 0, k) if end and m == 2 else R(pb, m * k, m * k + k),
                   ([(M("I256"), R("DEAD", c, c + k))] if t else []) + sel("B1", "AB", E * m + u, n))
                if m == 2 - end:
                    j = m + 1
                    act(at("SG", 0, j), R(pb, 0, j * k), AF.Sign, cc(10), -1.0)
                    mm(R(pb, 0, j * k), [(M("I"), at("AT", 0, j)), (M("IB"), at("SG", 0, j))])
                    tt(at("SC", 0, j), R(pb, 0, j * k), at("PO", 0, j), AL.add)
                    tt(R("M01", c, c + k), at("SC", 0, 1), at("SC", 1, 2), AL.max)
            if end:
                ts(R("NR", 0, k), R(pl, 0, k), cc(10), AL.is_lt, 2048.0, AL.mult)
                tt(at("SC", 2, 3), R("NR", 0, k), at("PO", 2, 3), AL.add)
            tt(R("MX", c, c + k), R("M01", c, c + k), at("SC", 2, 3), AL.max)
            u += n
        ts(W("KEY"), W("MX"), 8, AL.logical_shift_right, 15, AL.bitwise_and)
        for o in range(8):
            ts(R("IB", 50 * o + 1, 50 * o + 49), W("KEY"), float(8 + o), AL.is_equal)
        scan(W("S1"), W("M50"), W("IB"), AL.mult, AL.add)
        ts(R("CT", 0, 48), W("MX"), 2047, AL.bitwise_and)
        p1, p2 = R(bank(), 0, 400), R(bank(), 0, 400)
        mm(p1, [(M("DI"), R("ONE", 0, 400))], True, False)
        mm(p2, [(M("nU"), W("IB")), (M("I4k"), W("IB"))], True, False)
        mm(p1, [(M("nBOk"), W("S1"))], False, True)
        mm(p2, [(M("BO"), W("S1"))], False, True)
        act(W("RM"), p2, AF.Relu, -4096.0, 1.0)
        scan(W("S2"), W("C50"), p1, AL.min, AL.max)
        s2 = R("S2", 49, 400, 50)
        ts(W("L1"), s2, 0.25, AL.add)
        tt(W("EE"), IND(W("RM"), W("L1")), W("KI"), AL.is_equal)
        tt(W("L2F"), s2, R("C50", 0, 400, 50), AL.subtract)
        ts(W("L2"), W("L2F"), -0.75, AL.add)
        tt(R("CV", 128, 256), IND(W("VT"), W("L1")), W("EE"), AL.mult)
        tt(R("CV", 0, 128), IND(W("CT"), W("L2")), W("EE"), AL.mult)
        pb = bank()
        mm(R(pb, 0, 16), sel("B1", "CV", 0, 256))
        ts(W("SL"), R(pb, 0, 16), 0.25, AL.add)
        cl, vl = R("SL", 0, 8), R("SL", 8, 16)
        pv = bank()
        if "t" not in plan["scalar"]:
            mm(R(pv, 0, 128), [(M("BO"), R("CV", 128, 256))])
            act(W("VR"), R(pv, 0, 128), AF.Identity, float(S - E - 1024), 1.0)
        for b in range(2):
            tt(R("KE", 128 * b, 128 * b + 128), IND(R("KN", 112 * t + 56 * b, 112 * t + 56 * b + 56), W("L2")), W("EE"), AL.mult)
        xw = R("X", nw, nw + 2 * E)
        act(W("OH"), IND(xw, vl), AF.Identity, 110.0 - UP / 2, 0.5)
        if "r" in plan["scalar"]:
            act(W("RG"), IND(W("RT"), cl), AF.Identity, UP - 110.25, 0.5)
        else:
            ts(W("RG"), IND(W("RT"), cl), 0.5, AL.mult, UP - 110.25, AL.add)
        tt(IND(xw, vl), W("OH"), W("RG"), AL.add)
        ts(R("U", 0, 128), W("OH"), 2.0, AL.mult, -220.0, AL.add)
        if t + 1 < RO:
            pb = bank()
            mm(R(pb, 0, 48), [(M("I"), W("DC"))], True, False)
            for c6 in range(6):
                mm(R(pb, c6, 48, 6), [(M("nBO6"), R("S1", 48, 400, 50))], False, c6 == 5)
            act(W("DEAD"), R(pb, 0, 48), AF.Relu, 1.0, 1.0)
        act(W("Z0"), IND(W("QT"), cl), AF.Identity, 15.0, 2048.0)
        pz, pu = bank(), bank()
        old = [R("KE", 0, 128), R("KE", 128, 256)]
        mm(R(pz, 0, 128), [(M("I"), R("CZ", 128 * t, 128 * t + 128)), (M("I"), W("Z0"))])
        mm(R(pu, 0, 128), [(M("I4k"), W("N4")), (M("L0"), old[0]), (M("L1"), old[1]), (M("nIq"), W("Z0"))])
        if "t" in plan["scalar"]:
            act(W("TT"), IND(W("QT"), cl), AF.Identity, float(S - E - 1024), 1.0)
            mm(R(pv, 0, 128), [(M("BO"), R("CV", 128, 256)), (W("IF"), W("TT"))])
            if t == 0:
                ts(W("VR"), R(pv, 0, 128), -1024.5, AL.is_lt, float(S), AL.mult)
                tt(W("T2"), R(pv, 0, 128), W("VR"), AL.add)
            else:
                act(W("T2"), R(pv, 0, 128), AF.Copy)
            back = W("T2")
        else:
            tt(W("TT"), IND(W("QT"), cl), W("VR"), AL.add)
            back = W("TT")
            if t == 0:
                pw = bank()
                ts(R(pw, 0, 128), W("TT"), -1024.5, AL.is_lt, float(S), AL.mult)
                tt(W("T2"), R(pw, 0, 128), W("TT"), AL.add)
                back = W("T2")
        tt(W("N1"), R(pz, 0, 128), back, AL.max)
        tt(W("N2"), R(pu, 0, 128), W("N1"), AL.max)
        def spread(b, co, src):
            us = (((0, ""), (1, ""), (2, "a")), ((2, "b"), (3, ""), (4, ""), (5, "c")), ((5, "d"), (6, ""), (7, "")))[co]
            return [(M("K%d%s" % (b, x), 16 - (6 * u - 16 * co)), R(src, u, 128, 8)) for u, x in us]

        cp(W("G"), IND(W("NTB"), cl))
        for w in range(6):
            ts(R("U", 128 * w + 128, 128 * w + 256), W("G"), 4 * w, AL.logical_shift_right, 15, AL.bitwise_and)
        ts(W("N3"), W("Z0"), -12288.0 * 2048.0, AL.is_gt, cc(11), AL.mult)
        pf = bank()
        for co in range(3):
            mm(R(pf, co, 48, 3), [(M("I"), R("KD", co, 48, 3))] + spread(0, co, "N3"))
        ts(W("NL"), R(pf, 0, 48), -127.75, AL.add)
        u = 0
        for n in plan["nodes"]:
            act(R("X", O + S + u, O + S + u + n), IND(W("U"), R("NL", u // 16, (u + n) // 16)), AF.Identity, UP, 1.0)
            u += n
        pn = bank()
        for b in range(2):
            for co in range(3):
                mm(R(pn, 48 * b + co, 48 * b + 48, 3), spread(b, co, "N2"))
        ts(R("LK", kc + 96, kc + 192), R(pn, 0, 96), 1024.25 + O, AL.add)
        if t + 1 < RO:
            for b in range(2):
                act(R("KN", 112 + 56 * b, 160 + 56 * b), R(pn, 48 * b, 48 * b + 48), AF.Copy)
        p1, p2 = bank(), bank()
        step = [(M("L0"), old[0]), (M("L1"), old[1]), (M("nD"), W("N2")), (M("A3"), W("N2"))]
        mm(R(p1, 0, 128), step)
        mm(R(p2, 0, 128), step, True, False)
        act(W("HI"), R(p1, 0, 128), AF.Copy)
        mm(R(p2, 0, 128), [(M("A3"), W("HI"))], False, True)
        act(W("NB"), R(p2, 0, 128), AF.Copy)
        dk = E * (RO - 1 - t)
        cp(IND(R("DK", dk, dk + 2 * E), vl), W("NB"))
        pk = bank()
        for b in range(2):
            kn = 112 * t + 56 * b
            mm(R(pk, 48 * b, 48 * b + 48), [(W("IF"), R("KN", kn, kn + 48))] + sel("B%dr" % b, "DK", dk, E))
        ts(R("LK", kc, kc + 96), R(pk, 0, 96), 1024.25 + O, AL.add)
        row[0] = "rest%d" % t
        stage2(0, S, plan["rest"][t], t)
        row[0] = "next%d" % t
        stage1(0, S, plan["early"][t])
        stage1(S, S + E, plan["lnew"][t])
        stage1(S - E, S + E, plan["lold"][t])
    row[0] = "last"
    last(plan["last"])
    return ops


def depend(ops):
    hist = {}
    for n, op in enumerate(ops):
        dep = {}
        for kind, rs in (("r", op["rd"]), ("w", op["wr"])):
            for r in rs:
                ps = r[0].startswith("ps")
                for k, kk, a, b in hist.get(r[0], []):
                    if k == n:
                        continue
                    other = ops[k]
                    same = other["eng"] == op["eng"] and "sem" not in other and "sem" not in op
                    hit = a < r[2] and r[1] < b
                    if ps and not same:
                        dep[k] = True
                    elif hit and (kind == "w" or kk == "w"):
                        wait = (not same) or op["eng"] != "p"
                        dep[k] = dep.get(k, False) or wait
                    elif ps and op["eng"] == "p":
                        dep[k] = dep.get(k, False)
        for kind, rs in (("r", op["rd"]), ("w", op["wr"])):
            for r in rs:
                h = hist.setdefault(r[0], [])
                if kind == "w" and r[3] == 1 and not r[0].startswith("ps"):
                    h[:] = [e for e in h if not (r[1] <= e[2] and e[3] <= r[2])]
                elif r[0].startswith("ps"):
                    h[:] = h[-40:]
                h.append((n, kind, r[1], r[2]))
        op["dep"] = dep
    last = {}
    for n, op in enumerate(ops):
        row = op["kind"] in ("send", "load") or op.get("row")
        if row:
            if (op["eng"], row) in last:
                op["dep"].setdefault(last[op["eng"], row], False)
            last[op["eng"], row] = n
    for op in ops:
        if op["kind"] == "arrive":
            for n, o2 in enumerate(ops):
                if o2["kind"] == "send" and o2["args"][0] == op["args"][0]:
                    op["dep"][n] = True


def order(ops, C, plan):
    n = len(ops)
    cost = [op["cost"] for op in ops]
    eng = [op["eng"] for op in ops]
    tail = [0.0 if op["kind"] == "send" else op["lat"] for op in ops]
    early = [tail[k] + op["at"] for k, op in enumerate(ops)]
    after = [[] for _ in range(n)]
    before = [[] for _ in range(n)]
    slow = [[] for _ in range(n)]
    for c, op in enumerate(ops):
        for k, wait in op["dep"].items():
            gap = 0.0
            if wait:
                gap = ops[k]["lat"] + (C["same"] if eng[c] == eng[k] and "sem" not in ops[k] else C["hop"])
            after[k].append((c, gap))
            more = C["margin"] if wait and ops[k]["kind"] == "send" else 0.0
            before[c].append((k, gap + more))
            slow[k].append((c, gap + more))

    uses = {}
    for k, op in enumerate(ops):
        for r in op["rd"] + op["wr"]:
            if r[0].startswith("ps") and k not in uses.setdefault(r[0], []):
                uses[r[0]].append(k)
    opens = {ks[0]: name for name, ks in uses.items()}
    inside = {k: name for name, ks in uses.items() for k in ks}
    caps = dict(zip("ADLZ", plan["banks"]))

    def lay(nexts, prevs, ready, way, banks):
        left = [len(p) for p in prevs]
        ready = list(ready)
        free, pool, seq = {}, {}, {}
        start = [0.0] * n
        idle = {b: (0.0, None) for b in range(8)}
        held, todo, place = {}, {name: len(ks) for name, ks in uses.items()}, {}
        lists = sum(name[2] in "AL" for name in uses)
        shut = {kind: [k for k, name in opens.items() if name[2] == kind] for kind in caps}

        def due(k):
            if not banks or k not in opens:
                return ready[k]
            kind = opens[k][2]
            keep = (5 if lists else 2) if kind == "Z" else 0
            ahead = sum(way[j] > way[k] for j in shut[kind])
            if len(idle) <= keep or sum(name[2] == kind for name in held) + ahead >= caps[kind]:
                return None
            return max(ready[k], min(t for t, _ in idle.values()))

        for k in range(n):
            if left[k] == 0:
                pool.setdefault(eng[k], []).append(k)
        for _ in range(n):
            best = None
            for e, p in pool.items():
                at = {k: due(k) for k in p}
                at = {k: t for k, t in at.items() if t is not None}
                if not at:
                    continue
                now = max(free.get(e, 0.0), min(at.values()))
                k = max((k for k in at if at[k] <= now), key=lambda j: way[j])
                for j in at:
                    if at[j] > now and way[j] - way[k] > plan["patience"] and at[j] - now < plan["near" if e in "vs" else "wide"] * cost[k]:
                        k = j
                st = max(now, at[k])
                if best is None or st < best[0]:
                    best = (st, e, k)
            st, e, k = best
            pool[e].remove(k)
            seq.setdefault(e, []).append(k)
            free[e] = st + cost[k]
            start[k] = st
            if banks and k in inside:
                name = inside[k]
                if k in opens:
                    b = min(idle, key=lambda j: idle[j][0])
                    place[name] = (b, idle.pop(b)[1])
                    held[name] = 0.0
                    shut[name[2]].remove(k)
                held[name] = max(held[name], free[e] + C["hop"])
                todo[name] -= 1
                if todo[name] == 0:
                    idle[place[name][0]] = (held.pop(name), name)
                    lists -= name[2] in "AL"
            for c, gap in nexts[k]:
                ready[c] = max(ready[c], free[e] + gap)
                left[c] -= 1
                if left[c] == 0:
                    pool.setdefault(eng[c], []).append(c)
        return seq, start, place

    way = [-1.0] * n
    todo = list(range(n - 1, -1, -1))
    while todo:
        rest = []
        for k in todo:
            if any(way[c] < 0 for c, _ in after[k]):
                rest.append(k)
            else:
                way[k] = cost[k] + max([way[c] + gap for c, gap in slow[k]] + [early[k]])
        todo = rest
    best = None
    for _ in range(plan["turns"]):
        seq, start, place = lay(after, before, [0.0] * n, way, True)
        end = max(start[k] + cost[k] + tail[k] for k in range(n))
        if best is None or end < best[1]:
            best = (seq, end, start, place)
        back = lay(before, after, early, [start[k] + cost[k] for k in range(n)], False)[1]
        way = [back[k] + cost[k] for k in range(n)]
    for k in range(n):
        ops[k]["st"] = best[2][k]
    for name, (b, was) in best[3].items():
        for k in uses.get(was, []):
            first = uses[name][0]
            ops[first]["dep"][k] = ops[first]["dep"].get(k, False) or not (eng[k] == eng[first] == "p")
    return best[0], best[1], {name: "ps%d" % b for name, (b, _) in best[3].items()}


def order2(ops, C, plan):
    n = len(ops)
    cost = [op["cost"] for op in ops]
    eng = [op["eng"] for op in ops]
    tail = [0.0 if op["kind"] == "send" else op["lat"] for op in ops]
    early = [tail[k] + op["at"] for k, op in enumerate(ops)]
    after = [[] for _ in range(n)]
    before = [[] for _ in range(n)]

    def edge(k, c, wait):
        gap = ops[k]["lat"] + (C["same"] if eng[c] == eng[k] and "sem" not in ops[k] else C["hop"]) if wait else 0.0
        after[k].append((c, gap))
        before[c].append((k, gap))

    for c, op in enumerate(ops):
        for k, wait in op["dep"].items():
            edge(k, c, wait)
    uses = {}
    for k, op in enumerate(ops):
        for r in op["rd"] + op["wr"]:
            if r[0].startswith("ps") and k not in uses.setdefault(r[0], []):
                uses[r[0]].append(k)

    def lay(nexts, prevs, ready, way):
        start = [0.0] * n
        busy = {}
        left = [len(p) for p in prevs]
        pool = [k for k in range(n) if left[k] == 0]
        while pool:
            k = max(pool, key=lambda j: way[j])
            pool.remove(k)
            t = max([ready[k]] + [start[j] + cost[j] + gap for j, gap in prevs[k]])
            line = busy.setdefault(eng[k], [])
            i = 0
            for a, b in line:
                if t + cost[k] <= a:
                    break
                t = max(t, b)
                i += 1
            line.insert(i, (t, t + cost[k]))
            start[k] = t
            for c, _ in nexts[k]:
                left[c] -= 1
                if left[c] == 0:
                    pool.append(c)
        return start

    def banks(start):
        line = sorted((start[k], k) for k in range(n) if eng[k] == "p")
        for name in sorted(uses, key=lambda m: -start[uses[m][0]]):
            k = uses[name][0]
            if eng[k] == "p":
                t = min(start[c] - gap for c, gap in after[k]) - cost[k]
                line.remove((start[k], k))
                for a, j in reversed(line):
                    if a + cost[j] <= t:
                        break
                    if a < t + cost[k]:
                        t = a - cost[k]
                start[k] = max(t, start[k])
                line.append((start[k], k))
                line.sort()
        idle = {b: (0.0, None) for b in range(8)}
        place = {}
        for name in sorted(uses, key=lambda m: start[uses[m][0]]):
            b = min(idle, key=lambda j: idle[j][0])
            if idle[b][0] > start[uses[name][0]] + 1e-6:
                return None, (name, [m for _, m in idle.values()])
            place[name] = (b, idle[b][1])
            idle[b] = (max(start[k] + cost[k] for k in uses[name]) + C["hop"], name)
        return place, None

    way = [0.0] * n
    for k in sorted(range(n), key=lambda j: -lay(after, before, [0.0] * n, way)[j] if False else -j):
        way[k] = cost[k] + max([way[c] + gap for c, gap in after[k]] + [early[k]])
    for _ in range(3):
        for k in range(n - 1, -1, -1):
            way[k] = cost[k] + max([way[c] + gap for c, gap in after[k]] + [early[k]])
    best = None
    for turn in range(plan["turns"]):
        while True:
            start = lay(after, before, [0.0] * n, way)
            place, clash = banks(start)
            if clash is None:
                break
            name, held = clash
            late = min(held + [name], key=lambda m: way[uses[m][0]])
            done = min((m for m in held + [name] if m != late), key=lambda m: max(start[k] + cost[k] for k in uses[m]))
            for k in uses[done]:
                edge(k, uses[late][0], True)
        end = max(start[k] + cost[k] + tail[k] for k in range(n))
        if best is None or end < best[1]:
            best = (start, end, place)
        back = lay(before, after, early, [start[k] + cost[k] for k in range(n)])
        way = [back[k] + cost[k] for k in range(n)]
    seq = {}
    for k in sorted(range(n), key=lambda j: (best[0][j], j)):
        ops[k]["st"] = best[0][k]
        seq.setdefault(eng[k], []).append(k)
    for name, (b, was) in best[2].items():
        for k in uses.get(was, []):
            first = uses[name][0]
            ops[first]["dep"][k] = ops[first]["dep"].get(k, False) or not (eng[k] == eng[first] == "p")
    return seq, best[1], {name: "ps%d" % b for name, (b, _) in best[2].items()}


def hands(T, topo, rank):
    me = T.cores[rank]
    far = [c for c in topo.cores_of(me) if topo.die(c) != topo.die(me)]
    near = [c for c in topo.cores_of(me) if topo.die(c) == topo.die(me) and c != me]
    share = {"RT": ((me, 4), (far[2], 2), (far[3], 1)),
             "QT": ((far[0], 2), (near[0], 2), (far[1], 2), (near[1], 1)),
             "NTB": ((far[2], 2), (near[2], 2), (far[3], 1), (near[1], 2))}
    out = {}
    for turn, (name, parts) in enumerate(share.items()):
        dst = [T.cores[(rank + 1 + (j + 2 * turn) % (len(T.cores) - 1)) % len(T.cores)] for j in range(len(T.cores) - 1)]
        out[name] = []
        for c, k in parts:
            out[name].append((c, dst[:k]))
            dst = dst[k:]
    return out


def bits(es):
    m = 0
    for e in es:
        m |= 1 << e
    return m


def dst_id(topo, dst, src):
    rid, pid = topo.addr(dst, src)
    return DstId(rid=rid, pnc=pid)


def transfer(T, topo, core, name, rank, to, es, sem):
    part = T[name][:, rank * NT:rank * NT + NT]
    return RemoteDMATransfer(dst_ids=[dst_id(topo, c, core) for c in to], dma_engine_mask=bits(es), remote_sem=T.sem[sem + name],
                             src=part, dsts=[part] * len(to))


def folder(topo, me, j):
    near = [c for c in topo.cores_of(me) if topo.die(c) == topo.die(me) and c != me]
    return near[j % len(near)]


LAID = {}


def laid(rank):
    if rank not in LAID:
        ops = build(rank, COST, PLAN)
        depend(ops)
        seq, _, banks = order(ops, COST, PLAN)
        LAID[rank] = (ops, seq, banks)
    return LAID[rank]


def helper(g, core, T, topo):
    for rank, me in enumerate(T.cores):
        if core in topo.cores_of(me):
            used = 0
            for name, parts in hands(T, topo, rank).items():
                for c, to in parts:
                    if c == core:
                        es = topo.engines(core, to[0])
                        g.wait_ge(T.sem["hand_" + name], len(es))
                        g.remote_dma_fused([transfer(T, topo, core, name, rank, to, es, "in_")], local_sem=T.sem.sent)
                        used += len(es)
            ops, seq, _ = laid(rank)
            es = topo.engines(core, me)
            for k in seq["g"]:
                if ops[k]["kind"] == "fold" and folder(topo, me, ops[k]["args"][2]) == core:
                    name, a, b, _ = ops[k]["args"][0]
                    j = ops[k]["args"][2]
                    g.wait_ge(T.sem["fold%d" % j], len(es))
                    rid, pid = topo.addr(me, core)
                    g.remote_dma(T[name][:, a:b], T[name][:, a:b], T.sem["back%d" % j], T.sem.sent, pid, rid, bits(es))
                    used += len(es)
            g.wait_ge(T.sem.sent, used)


def rank_program(g, core, T, topo):
    rank = T.rank_of(core)
    if rank is None:
        helper(g, core, T, topo)
        return
    ops, seq, banks = laid(rank)
    Q = {"v": g.vector, "s": g.scalar, "p": g.tensor, "g": g, "y": g.sync}
    handed = hands(T, topo, rank)
    peers = [c for c in T.cores if c != core]
    off = topo.engines(core, peers[0])
    spare = [e for e in topo.engines(core, handed["NTB"][0][0]) if e not in off]

    def ap(r):
        if not isinstance(r, tuple):
            return r
        if r[0] == "@":
            return ap(r[1]).indirect(ap(r[2]))
        buf = T[banks.get(r[0], r[0])]
        return buf[:, r[1]:r[2]:r[3]] if r[3] != 1 else buf[:, r[1]:r[2]]

    needed = set()
    for op in ops:
        for d, wait in op["dep"].items():
            if wait:
                needed.add(d)
    count = {}
    total = {}
    for e, ks in seq.items():
        if e in ESEM:
            cs = [k for k in ks if "sem" not in ops[k] and ops[k]["kind"] != "send"]
            needed.add(cs[-1])
            c = 0
            for k in cs:
                if k in needed:
                    c += 1
                    count[k] = (ESEM[e], c)
            total[ESEM[e]] = c
    for k, op in enumerate(ops):
        if op["kind"] == "arrive":
            count[k] = (op["sem"], len(off) * len(peers))
        elif "sem" in op:
            count[k] = (op["sem"], 16)
        if "sem" in op:
            total[count[k][0]] = count[k][1]
    sent = [0]

    def send(name):
        cores = [c for c, _ in handed[name] if c != core]
        direct = [to for c, to in handed[name] if c == core]
        if direct:
            trs = [transfer(T, topo, core, name, rank, direct[0], off, "in_"), transfer(T, topo, core, name, rank, cores, spare, "hand_")]
        else:
            trs = [transfer(T, topo, core, name, rank, cores[1::2], off, "hand_"), transfer(T, topo, core, name, rank, cores[::2], spare, "hand_")]
        g.remote_dma_fused(trs, local_sem=T.sem.sent)
        sent[0] += len(off) + len(spare)

    for e, ks in seq.items():
        if e == "x":
            continue
        q = Q[e]
        seen = {}
        for k in ks:
            op = ops[k]
            want = {}
            for d, wait in op["dep"].items():
                if wait:
                    s, c = count[d]
                    want[s] = max(want.get(s, 0), c)
            for s, c in want.items():
                if seen.get(s, 0) < c:
                    q.wait_ge(T.sem[s], c)
                    seen[s] = c
            a = op["args"]
            kind = op["kind"]
            if kind == "send":
                send(*a)
                continue
            if kind == "fold":
                tr = RemoteDMATransfer(dst_ids=[dst_id(topo, folder(topo, core, a[2]), core)], dma_engine_mask=bits(off + spare),
                                       remote_sem=T.sem["fold%d" % a[2]], srcs=[ap(r) for r in a[1]], dsts=[ap(a[0])], alu_op=2)
                g.remote_dma_fused([tr], local_sem=T.sem.sent)
                sent[0] += len(off + spare)
                continue
            if kind == "load":
                q.dma_start(ap(a[0]), T[a[1][0]][:]).then_inc(T.sem[op["sem"]], 16)
                continue
            if kind == "store":
                q.dma_start(T.y[:, a[1][1]:a[1][2]], ap(a[0])).then_inc(T.sem[op["sem"]], 16)
                continue
            if kind == "ts":
                if a[5] is None:
                    ins = q.tensor_scalar(ap(a[0]), ap(a[1]), ap(a[2]), None, a[4])
                else:
                    ins = q.tensor_scalar(ap(a[0]), ap(a[1]), ap(a[2]), ap(a[3]), a[4], a[5])
            elif kind == "tt":
                ins = q.tensor_tensor(ap(a[0]), ap(a[1]), ap(a[2]), a[3])
            elif kind == "cp":
                ins = q.tensor_copy(ap(a[0]), ap(a[1]))
            elif kind == "scan":
                ins = q.tensor_tensor_scan(ap(a[0]), ap(a[1]), ap(a[2]), a[3], a[4], a[5])
            elif kind == "ms":
                ins = q.memset(ap(a[0]), a[1])
            elif kind == "act":
                if a[2] == AF.Copy:
                    ins = q.activation(ap(a[0]), ap(a[1]), a[2], scale=ap(a[4]))
                else:
                    ins = q.activation(ap(a[0]), ap(a[1]), a[2], bias=ap(a[3]), scale=ap(a[4]))
            elif kind == "mm":
                for j, (l, r) in enumerate(a[1]):
                    ins = q.matmul(ap(a[0]), ap(l), ap(r), a[2] and j == 0, a[3] and j == len(a[1]) - 1)
            elif kind == "sel":
                ins = q.affine_select(ap(a[0]), ap(a[1]), a[2], a[3], a[4], a[5], a[6])
            elif SCRATCH[a[0][0]][2] == I32:
                ins = q.iota(ap(a[0]), a[1], a[2], a[3])
            else:
                ins = q.iota(ap(a[0]), a[1], a[2], a[3], allow_small_or_imprecise_dtypes=True)
            if k in count:
                ins.then_inc(T.sem[count[k][0]], 1)
    g.wait_ge(T.sem.sent, sent[0])
    for s, c in total.items():
        g.sync.wait_ge(T.sem[s], c)
